import numpy as np
import ml_dtypes


def mxq(x, axis, fmt="e4m3"):
    dtype, down = {"e4m3": (ml_dtypes.float8_e4m3fn, 7), "e5m2": (ml_dtypes.float8_e5m2, 14)}[fmt]
    v = np.moveaxis(np.asarray(x, np.float32).astype(ml_dtypes.bfloat16).astype(np.float64), axis, -1)
    blocks = v.reshape(v.shape[:-1] + (-1, 32))
    amax = np.abs(blocks).max(-1, keepdims=True)
    byte = np.maximum(np.where(amax > 0, np.frexp(amax)[1] - 1 + 127, 0) - down, 1)
    scale = np.exp2(byte - 127.0)
    codes = (blocks / scale).astype(np.float32).astype(dtype).astype(np.float64)
    return np.moveaxis((codes * scale).reshape(v.shape), -1, axis)


WIDE = False


def mx_kscale(k):
    if not WIDE:
        return np.ones(k)
    levels = np.array([10, -10, 5, -5, 0])
    if k % 512:
        return np.exp2(np.random.permutation(np.resize(levels, k // 32))).repeat(32)
    a = np.empty((k // 512, 16))
    for p in range(k // 512):
        a[p, :8] = np.random.permutation(np.resize(levels, 8))
        for g in range(8):
            far = levels[np.abs(levels - a[p, g]) >= 10]
            a[p, g + 8] = far[np.random.randint(len(far))]
    return np.exp2(a.ravel()).repeat(32)


def f64(x):
    return np.asarray(x).astype(np.float64)


def striped(idx):
    return np.tile(idx.reshape(-1, 16).T, (8, 1)).astype(np.uint16)


def unstriped(offs):
    return offs[:16].T.reshape(-1).astype(np.int64)


E2M1 = np.array([0.0, 0.5, 1.0, 1.5, 2.0, 3.0, 4.0, 6.0, -0.0, -0.5, -1.0, -1.5, -2.0, -3.0, -4.0, -6.0])


def pack_weight(w, fmt):
    k, n = w.shape
    w = f64(np.asarray(w, np.float32).astype(ml_dtypes.bfloat16)).reshape(k // 32, 32, n)
    amax = np.abs(w).max(1)
    if fmt == "e4m3":
        byte = np.frexp(amax)[1] - 1 + 127 - 7
    else:
        mant, ex = np.frexp(amax / 6.0)
        byte = np.where(mant > 0.5, ex, ex - 1) + 127
    byte = np.clip(np.where(amax > 0, byte, 1), 1, 254)
    scaled = (w * np.exp2(127.0 - byte)[:, None, :]).reshape(k, n).astype(np.float32)
    by_word = np.ascontiguousarray(scaled.reshape(k // 512, 128, 4, n).transpose(0, 1, 3, 2))
    if fmt == "e4m3":
        words = by_word.astype(ml_dtypes.float8_e4m3fn).view(np.uint8)
    else:
        c = by_word.astype(ml_dtypes.float4_e2m1fn).view(np.uint8) & 0xF
        words = (c[..., 0::2] | (c[..., 1::2] << 4)).reshape(k // 512, 128, 2 * n)
    return np.ascontiguousarray(words), np.ascontiguousarray(byte.astype(np.uint8).reshape(k // 512, 16, n))


def unpack_weight(words, scales, fmt):
    g, _, n = scales.shape
    words = np.ascontiguousarray(words).reshape(g, 128, n, -1)
    if fmt == "e4m3":
        vals = words.view(ml_dtypes.float8_e4m3fn).astype(np.float64)
    else:
        nib = np.empty((g, 128, n, 4), np.uint8)
        nib[..., 0::2] = words & 0xF
        nib[..., 1::2] = words >> 4
        vals = E2M1[nib]
    vals = vals * np.repeat(np.exp2(scales.astype(np.float64) - 127.0), 8, axis=1)[..., None]
    return vals.transpose(0, 1, 3, 2).reshape(g * 512, n)


def gelu(v):
    return 0.5 * v * (1.0 + np.tanh(np.sqrt(2.0 / np.pi) * (v + 0.044715 * v**3)))


K, T, S, H, H2, P, N = 1024, 4096, 1024, 512, 1024, 512, 768

def setup_inputs():
    n = np.random.standard_normal
    s = mx_kscale(K)[:, None]
    u = mx_kscale(H)[:, None]
    tab_words, tab_scales = pack_weight(n((K, T)) * s, "e4m3")
    w1 = n((K, H2)) / np.sqrt(K) / s
    w1[:, H:] = w1[:, H:] * u.T
    wev_words, wev_scales = pack_weight(n((H, N)) / np.sqrt(H) / u, "e4m3")
    wvol_words, wvol_scales = pack_weight(n((H, N)) / np.sqrt(H) / u, "e2m1")
    return {
        "tab_words": tab_words, "tab_scales": tab_scales,
        "offs": striped(np.random.permutation(T)[:S]),
        "pos1": striped(np.random.permutation(S)[:P]),
        "pos2": striped(np.random.permutation(S)[:P]),
        "pos3": striped(np.random.permutation(S)[:P]),
        "w1": w1.astype(np.float32),
        "wev_words": wev_words, "wev_scales": wev_scales,
        "wvol_words": wvol_words, "wvol_scales": wvol_scales,
    }

def reference(tab_words, tab_scales, offs, pos1, pos2, pos3, w1, wev_words, wev_scales, wvol_words, wvol_scales):
    v = unpack_weight(tab_words, tab_scales, "e4m3")[:, unstriped(offs)]
    h = mxq(f64(w1), 0, "e4m3").T @ v
    day = h[:H]
    carry = h[H:]
    z = (np.tanh(day[:, unstriped(pos1)]) - day[:, unstriped(pos2)]) * carry[:, unstriped(pos3)]
    zq = mxq(z, 0, "e4m3")
    evidence = unpack_weight(wev_words, wev_scales, "e4m3").T @ zq
    volume = unpack_weight(wvol_words, wvol_scales, "e2m1").T @ zq
    return evidence / (1.0 + np.abs(volume))

@@ -1,0 +1,216 @@
+from contextlib import ExitStack
+
+import concourse.mybir as mybir
+
+K, T, S, H, M, N = 1024, 4096, 1024, 512, 512, 768
+FLOPS = 2 * K * 2 * H * S + 2 * 2 * H * N * M
+
+F32 = mybir.dt.float32
+BF16 = mybir.dt.bfloat16
+I32 = mybir.dt.int32
+U32 = mybir.dt.uint32
+U16 = mybir.dt.uint16
+U8 = mybir.dt.uint8
+FP8X4 = mybir.dt.float8_e4m3fn_x4
+FP4X4 = mybir.dt.float4_e2m1fn_x4
+ACT = mybir.ActivationFunctionType
+ALU = mybir.AluOpType
+
+P = 128
+PACK = 4
+PASSES = K // (P * PACK)
+BANK = 512
+M_PART = 256
+
+
+def tile_list_skimming_triage_kernel(
+    tc, tab_words, tab_scales, offs, pos1, pos2, pos3, w1, wev_words, wev_scales, wvol_words, wvol_scales, out
+):
+    nc = tc.nc
+    with ExitStack() as ctx:
+        lists = ctx.enter_context(tc.tile_pool(name="lists", bufs=1))
+        keep = ctx.enter_context(tc.tile_pool(name="keep", bufs=1))
+        reuse = ctx.enter_context(tc.tile_pool(name="reuse", bufs=1))
+        ring = ctx.enter_context(tc.tile_pool(name="ring", bufs=3))
+        psum = ctx.enter_context(tc.psum_pool(name="psum", bufs=8))
+
+        offs_sb = lists.tile([P, S // 16], U16, name="offs_sb")
+        pos1_sb = lists.tile([P, M // 16], U16, name="pos1_sb")
+        pos2_sb = lists.tile([P, M // 16], U16, name="pos2_sb")
+        pos3_sb = lists.tile([P, M // 16], U16, name="pos3_sb")
+
+        tab = [reuse.tile([P, T], U32, name=f"tab{a}", align_bytes=64, offset=4 * T * a) for a in range(PASSES)]
+        tab_planes = reuse.tile([P, T], U8, name="tab_planes", align_bytes=64, offset=8 * T)
+        raw = [[keep.tile([P, PACK, H], F32, name=f"raw{c}{a}", align_bytes=64) for a in range(PASSES)] for c in range(2)]
+        wev = keep.tile([P, N], U32, name="wev", align_bytes=64)
+        wvol = keep.tile([P, 2 * N], U8, name="wvol", align_bytes=64)
+        wev_plane = keep.tile([P, N], U8, name="wev_plane", align_bytes=64)
+        wvol_plane = keep.tile([P, N], U8, name="wvol_plane", align_bytes=64)
+
+        def load_w1(c, a):
+            rows = w1[a * P * PACK : (a + 1) * P * PACK, c * H : (c + 1) * H]
+            nc.sync.dma_start(out=raw[c][a][:], in_=rows.rearrange("(p j) r -> p j r", j=PACK))
+
+        def load_tab(a):
+            nc.sync.dma_start(out=tab[a][:].bitcast(I32), in_=tab_words[a].rearrange("p t i -> p (t i)").bitcast(I32))
+
+        nc.vector.memset(tab_planes[:].bitcast(I32), 0)
+        for q in range(4):
+            nc.gpsimd.dma_start(
+                out=tab_planes[32 * q : 32 * q + 4 * PASSES, :].bitcast(I32),
+                in_=tab_scales[:, 4 * q : 4 * q + 4, :].bitcast(I32),
+            )
+        nc.sync.dma_start(offs_sb[:], offs)
+        load_w1(0, 0)
+        load_w1(0, 1)
+        load_tab(0)
+        load_tab(1)
+        nc.sync.dma_start(pos1_sb[:], pos1)
+        nc.sync.dma_start(pos2_sb[:], pos2)
+        nc.sync.dma_start(pos3_sb[:], pos3)
+        load_w1(1, 0)
+        load_w1(1, 1)
+        nc.vector.memset(wev_plane[:].bitcast(I32), 0)
+        nc.vector.memset(wvol_plane[:].bitcast(I32), 0)
+        nc.sync.dma_start(out=wev[:].bitcast(I32), in_=wev_words[0].rearrange("p c i -> p (c i)").bitcast(I32))
+        nc.sync.dma_start(out=wvol[:].bitcast(I32), in_=wvol_words[0].bitcast(I32))
+        for plane, scales in ((wev_plane, wev_scales), (wvol_plane, wvol_scales)):
+            for q in range(4):
+                nc.sync.dma_start(
+                    out=plane[32 * q : 32 * q + 4, :].bitcast(I32), in_=scales[0, 4 * q : 4 * q + 4, :].bitcast(I32)
+                )
+
+        big = keep.tile([P, 1], F32, name="big")
+        one = keep.tile([P, 1], F32, name="one")
+        nc.vector.memset(big[:], 64.0)
+        nc.scalar.activation(one[:], big[:], ACT.Sigmoid)
+
+        v_words = [
+            keep.tile([P, S], U32, name="v_words0", align_bytes=64),
+            reuse.tile([P, S], U32, name="v_words1", align_bytes=64, offset=8 * T),
+        ]
+        v_planes = keep.tile([P, S], U8, name="v_planes", align_bytes=64)
+        grouped = [
+            [keep.tile([P, PACK, P, PACK], BF16, name=f"grouped0{a}", align_bytes=64) for a in range(PASSES)],
+            [reuse.tile([P, PACK, P, PACK], BF16, name=f"grouped1{a}", align_bytes=64, offset=4 * T + T * a) for a in range(PASSES)],
+        ]
+        w_words = [[keep.tile([P, H], U32, name=f"w_words{c}{a}", align_bytes=64) for a in range(PASSES)] for c in range(2)]
+        w_plane = [[keep.tile([P, H], U8, name=f"w_plane{c}{a}", align_bytes=64) for a in range(PASSES)] for c in range(2)]
+
+        def group_w1(c, a, scalar_share):
+            src = raw[c][a][:].rearrange("p j (m t) -> p m j t", t=PACK)
+            dst = grouped[c][a][:].rearrange("p t m j -> p m j t")
+            if scalar_share:
+                nc.scalar.copy(dst[:, :scalar_share], src[:, :scalar_share])
+            nc.vector.tensor_copy(dst[:, scalar_share:], src[:, scalar_share:])
+
+        def quantize_w1(c, a):
+            flat = grouped[c][a][:].rearrange("p t m j -> p (t m j)")
+            nc.vector.quantize_mx(out=w_words[c][a][:].bitcast(FP8X4), scales=w_plane[c][a][:], in_=flat)
+
+        def stage1_pass(bank, c, a, t, half):
+            rows = slice(t * P, (t + 1) * P)
+            cols = slice(half * BANK, (half + 1) * BANK)
+            nc.tensor.matmul_mx(
+                out=bank[:],
+                lhsT=w_words[c][a][:, rows].bitcast(FP8X4),
+                lhsT_scale=w_plane[c][a][:, rows],
+                rhs=v_words[a][:, cols].bitcast(FP8X4),
+                rhs_scale=v_planes[4 * a :, cols],
+                start=(a == 0),
+                stop=(a == PASSES - 1),
+            )
+
+        h = [[keep.tile([P, S], F32, name=f"h{c}{t}", align_bytes=64) for t in range(PACK)] for c in range(2)]
+        places = [(t, half) for t in range(PACK) for half in range(2)]
+        by_half = [(t, half) for half in range(2) for t in range(PACK)]
+
+        for a in range(PASSES):
+            group_w1(0, a, 64)
+            quantize_w1(0, a)
+        nc.vector.tensor_copy(v_planes[:], tab_planes[:].indirect(offs_sb[:]))
+        nc.vector.tensor_copy(v_words[0][:], tab[0][:].indirect(offs_sb[:]))
+        for half in range(2):
+            nc.vector.tensor_copy(
+                v_words[1][:, half * BANK : (half + 1) * BANK],
+                tab[1][:].indirect(offs_sb[:, half * BANK // 16 : (half + 1) * BANK // 16]),
+            )
+        day_banks = {pl: psum.tile([P, BANK], F32, name="bank") for pl in places}
+        for a in range(PASSES):
+            for t, half in by_half:
+                stage1_pass(day_banks[t, half], 0, a, t, half)
+
+        for a in range(PASSES):
+            group_w1(1, a, 0)
+            quantize_w1(1, a)
+
+        sig = [keep.tile([P, M], F32, name=f"sig{t}", align_bytes=64) for t in range(PACK)]
+        th = [keep.tile([P, M], F32, name=f"th{t}", align_bytes=64) for t in range(PACK)]
+        diff = [keep.tile([P, M], F32, name=f"diff{t}", align_bytes=64) for t in range(PACK)]
+        for t in range(PACK):
+            for half in range(2):
+                cols = slice(half * BANK, (half + 1) * BANK)
+                if t == 3:
+                    nc.vector.tensor_copy(h[0][t][:, cols], day_banks[t, half][:])
+                else:
+                    nc.scalar.copy(h[0][t][:, cols], day_banks[t, half][:])
+            nc.scalar.activation(sig[t][:], h[0][t][:].indirect(pos1_sb[:]), ACT.Sigmoid, scale=2.0)
+            nc.vector.tensor_scalar(th[t][:], sig[t][:], 2.0, -1.0, ALU.mult, ALU.add)
+            nc.vector.tensor_tensor(diff[t][:], h[0][t][:].indirect(pos2_sb[:]), th[t][:], ALU.subtract)
+
+        for t, half in places:
+            bank = psum.tile([P, BANK], F32, name="bank")
+            for a in range(PASSES):
+                stage1_pass(bank, 1, a, t, half)
+            nc.scalar.copy(h[1][t][:, half * BANK : (half + 1) * BANK], bank[:])
+
+        one_again = keep.tile([P, 1], F32, name="one_again")
+        nc.scalar.activation(one_again[:], sig[PACK - 1][:, 0:1], ACT.Abs_reciprocal_sqrt, scale=0.0, bias=one[:])
+
+        pairs = BANK // M_PART
+        for part in range(M // M_PART):
+            cases = slice(part * M_PART, (part + 1) * M_PART)
+            list_cols = slice(part * M_PART // 16, (part + 1) * M_PART // 16)
+            neg_z = keep.tile([P, PACK, M_PART], F32, name=f"neg_z{part}", align_bytes=64)
+            for t in range(PACK):
+                nc.vector.tensor_tensor(neg_z[:, t, :], h[1][t][:].indirect(pos3_sb[:, list_cols]), diff[t][:, cases], ALU.mult)
+            z_bf = keep.tile([P, M_PART, PACK], BF16, name=f"z_bf{part}", align_bytes=64)
+            nc.vector.tensor_scalar(
+                z_bf[:].rearrange("p (c i) t -> p c t i", i=4),
+                neg_z[:].rearrange("p t (c i) -> p c t i", i=4),
+                -1.0, None, ALU.mult,
+            )
+            z_words = keep.tile([P, M_PART], U32, name=f"z_words{part}", align_bytes=64)
+            z_plane = keep.tile([P, M_PART], U8, name=f"z_plane{part}", align_bytes=64)
+            nc.vector.quantize_mx(out=z_words[:].bitcast(FP8X4), scales=z_plane[:], in_=z_bf[:].rearrange("p m t -> p (m t)"))
+            for g in range(N // P // pairs):
+                vol = psum.tile([P, BANK], F32, name="bank")
+                ev = psum.tile([P, BANK], F32, name="bank")
+                for i in range(pairs):
+                    n0 = (g * pairs + i) * P
+                    nc.tensor.matmul_mx(
+                        out=vol[:, i * M_PART : (i + 1) * M_PART],
+                        lhsT=wvol[:, 2 * n0 : 2 * (n0 + P)].bitcast(FP4X4), lhsT_scale=wvol_plane[:, n0 : n0 + P],
+                        rhs=z_words[:].bitcast(FP8X4), rhs_scale=z_plane[:], start=True, stop=True,
+                    )
+                for i in range(pairs):
+                    n0 = (g * pairs + i) * P
+                    nc.tensor.matmul_mx(
+                        out=ev[:, i * M_PART : (i + 1) * M_PART],
+                        lhsT=wev[:, n0 : n0 + P].bitcast(FP8X4), lhsT_scale=wev_plane[:, n0 : n0 + P],
+                        rhs=z_words[:].bitcast(FP8X4), rhs_scale=z_plane[:], start=True, stop=True,
+                    )
+                size = ring.tile([P, BANK], F32, name="size")
+                root = ring.tile([P, BANK], F32, name="root")
+                once = ring.tile([P, BANK], F32, name="once")
+                res = ring.tile([P, BANK], F32, name="res")
+                nc.scalar.activation(size[:], vol[:], ACT.Abs)
+                nc.scalar.activation(root[:], size[:], ACT.Abs_reciprocal_sqrt, bias=one_again[:])
+                if part == 0:
+                    nc.scalar.activation(once[:], root[:], ACT.Square)
+                    nc.vector.tensor_tensor(res[:], ev[:], once[:], ALU.mult)
+                else:
+                    nc.vector.tensor_tensor(once[:], ev[:], root[:], ALU.mult)
+                    nc.vector.tensor_tensor(res[:], once[:], root[:], ALU.mult)
+                rows = out[g * pairs * P : (g + 1) * pairs * P, cases]
+                nc.sync.dma_start(out=rows.rearrange("(i p) m -> p i m", p=P), in_=res[:].rearrange("p (i m) -> p i m", i=pairs))

@@ -21,6 +21,9 @@ PACK = 4
 PASSES = K // (P * PACK)
 BANK = 512
 M_PART = 256
+GROUP = BANK // M_PART
+KIB = 1024
+DAY, CARRY = 0, 1
 
 
 def tile_list_skimming_triage_kernel(
@@ -31,7 +34,7 @@ def tile_list_skimming_triage_kernel(
         lists = ctx.enter_context(tc.tile_pool(name="lists", bufs=1))
         keep = ctx.enter_context(tc.tile_pool(name="keep", bufs=1))
         reuse = ctx.enter_context(tc.tile_pool(name="reuse", bufs=1))
-        ring = ctx.enter_context(tc.tile_pool(name="ring", bufs=3))
+        ring = ctx.enter_context(tc.tile_pool(name="ring", bufs=4))
         psum = ctx.enter_context(tc.psum_pool(name="psum", bufs=8))
 
         offs_sb = lists.tile([P, S // 16], U16, name="offs_sb")
@@ -39,37 +42,102 @@ def tile_list_skimming_triage_kernel(
         pos2_sb = lists.tile([P, M // 16], U16, name="pos2_sb")
         pos3_sb = lists.tile([P, M // 16], U16, name="pos3_sb")
 
-        tab = [reuse.tile([P, T], U32, name=f"tab{a}", align_bytes=64, offset=4 * T * a) for a in range(PASSES)]
-        tab_planes = reuse.tile([P, T], U8, name="tab_planes", align_bytes=64, offset=8 * T)
-        raw = [[keep.tile([P, PACK, H], F32, name=f"raw{c}{a}", align_bytes=64) for a in range(PASSES)] for c in range(2)]
-        wev = keep.tile([P, N], U32, name="wev", align_bytes=64)
-        wvol = keep.tile([P, 2 * N], U8, name="wvol", align_bytes=64)
-        wev_plane = keep.tile([P, N], U8, name="wev_plane", align_bytes=64)
-        wvol_plane = keep.tile([P, N], U8, name="wvol_plane", align_bytes=64)
+        def placed(name, shape, dtype, kib):
+            return reuse.tile(shape, dtype, name=name, align_bytes=64, offset=kib * KIB)
 
-        def load_w1(c, a):
-            rows = w1[a * P * PACK : (a + 1) * P * PACK, c * H : (c + 1) * H]
-            nc.sync.dma_start(out=raw[c][a][:], in_=rows.rearrange("(p j) r -> p j r", j=PACK))
+        tab = [placed("tab0", [P, T], U32, 0), placed("tab1", [P, T], U32, 16)]
+        tab_rows = placed("tab_rows", [P, T], U8, 30)
+        raw_day1a = placed("raw_day1a", [P, PACK, H // 2], F32, 32)
+        raw_carry0 = placed("raw_carry0", [P, PACK, H], F32, 36)
+        raw_day0 = placed("raw_day0", [P, PACK, H], F32, 42)
+        raw_day1b = placed("raw_day1b", [P, PACK, H // 2], F32, 44)
+        raw_carry1 = placed("raw_carry1", [P, PACK, H], F32, 48)
+        wev = placed("wev", [P, N], U32, 0)
+        wvol = placed("wvol", [P, 2 * N], U8, 3)
+        wev_plane = placed("wev_plane", [P, N], U8, 5)
+        wvol_plane = placed("wvol_plane", [P, N], U8, 6)
+
+        def load_w1(raw, a, first):
+            rows = w1[a * P * PACK : (a + 1) * P * PACK, first : first + raw.shape[2]]
+            nc.sync.dma_start(out=raw[:], in_=rows.rearrange("(p j) r -> p j r", j=PACK))
 
         def load_tab(a):
             nc.sync.dma_start(out=tab[a][:].bitcast(I32), in_=tab_words[a].rearrange("p t i -> p (t i)").bitcast(I32))
 
-        nc.vector.memset(tab_planes[:].bitcast(I32), 0)
-        for q in range(4):
-            nc.gpsimd.dma_start(
-                out=tab_planes[32 * q : 32 * q + 4 * PASSES, :].bitcast(I32),
-                in_=tab_scales[:, 4 * q : 4 * q + 4, :].bitcast(I32),
-            )
+        v_words = [keep.tile([P, S], U32, name=f"v_words{a}", align_bytes=64) for a in range(PASSES)]
+        v_rows = keep.tile([P, S], U8, name="v_rows", align_bytes=64)
+        v_planes = keep.tile([P, PASSES * S], U8, name="v_planes", align_bytes=64)
+
+        nc.vector.memset(tab_rows[32:64, :].bitcast(I32), 0)
+        nc.vector.memset(tab_rows[64:128, :].bitcast(I32), 0)
+        nc.vector.memset(v_planes[:].bitcast(I32), 0)
         nc.sync.dma_start(offs_sb[:], offs)
-        load_w1(0, 0)
-        load_w1(0, 1)
-        load_tab(0)
-        load_tab(1)
+        for a in range(PASSES):
+            nc.sync.dma_start(out=tab_rows[a:32:PASSES, :].bitcast(I32), in_=tab_scales[a].bitcast(I32))
+        load_w1(raw_day0, 0, 0)
         nc.sync.dma_start(pos1_sb[:], pos1)
         nc.sync.dma_start(pos2_sb[:], pos2)
         nc.sync.dma_start(pos3_sb[:], pos3)
-        load_w1(1, 0)
-        load_w1(1, 1)
+        load_tab(0)
+        nc.vector.tensor_copy(v_rows[:], tab_rows[:].indirect(offs_sb[:]))
+        for q in range(4):
+            nc.sync.dma_start(
+                out=v_planes[32 * q : 32 * q + 4, :].bitcast(I32), in_=v_rows[8 * q : 8 * q + 8, :].bitcast(I32)
+            )
+        load_tab(1)
+        load_w1(raw_day1a, 1, 0)
+
+        big = keep.tile([P, 1], F32, name="big")
+        one = keep.tile([P, 1], F32, name="one")
+        nc.vector.memset(big[:], 64.0)
+        nc.scalar.activation(one[:], big[:], ACT.Sigmoid)
+
+        grouped = [[keep.tile([P, PACK, P, PACK], BF16, name=f"grouped{c}{a}", align_bytes=64) for a in range(PASSES)] for c in range(2)]
+        w_words = [[keep.tile([P, H], U32, name=f"w_words{c}{a}", align_bytes=64) for a in range(PASSES)] for c in range(2)]
+        w_plane = [[keep.tile([P, H], U8, name=f"w_plane{c}{a}", align_bytes=64) for a in range(PASSES)] for c in range(2)]
+
+        def group_w1(raw, c, a, first, scalar_share):
+            count = raw.shape[2] // PACK
+            src = raw[:].rearrange("p j (m t) -> p m j t", t=PACK)
+            dst = grouped[c][a][:].rearrange("p t m j -> p m j t")[:, first : first + count]
+            if scalar_share > 0:
+                nc.scalar.copy(dst[:, :scalar_share], src[:, :scalar_share])
+            if scalar_share < count:
+                nc.vector.tensor_copy(dst[:, scalar_share:], src[:, scalar_share:])
+
+        def quantize_w1(c, a, calls):
+            flat = grouped[c][a][:].rearrange("p t m j -> p (t m j)")
+            width = H // calls
+            for i in range(calls):
+                cols = slice(i * width, (i + 1) * width)
+                nc.vector.quantize_mx(
+                    out=w_words[c][a][:, cols].bitcast(FP8X4),
+                    scales=w_plane[c][a][:, cols],
+                    in_=flat[:, PACK * i * width : PACK * (i + 1) * width],
+                )
+
+        def stage1_pass(bank, c, a, t, half):
+            rows = slice(t * P, (t + 1) * P)
+            nc.tensor.matmul_mx(
+                out=bank[:],
+                lhsT=w_words[c][a][:, rows].bitcast(FP8X4),
+                lhsT_scale=w_plane[c][a][:, rows],
+                rhs=v_words[a][:, half * BANK : (half + 1) * BANK].bitcast(FP8X4),
+                rhs_scale=v_planes[:, a * S + half * BANK : a * S + (half + 1) * BANK],
+                start=(a == 0),
+                stop=(a == PASSES - 1),
+            )
+
+        h = [[keep.tile([P, S], F32, name=f"h{c}{t}", align_bytes=64) for t in range(PACK)] for c in range(2)]
+        places = [(t, half) for t in range(PACK) for half in range(2)]
+
+        group_w1(raw_day0, DAY, 0, 0, P)
+        quantize_w1(DAY, 0, 1)
+        load_w1(raw_day1b, 1, H // 2)
+        load_w1(raw_carry0, 0, H)
+        load_w1(raw_carry1, 1, H)
+        nc.vector.tensor_copy(v_words[0][:], tab[0][:].indirect(offs_sb[:]))
+
         nc.vector.memset(wev_plane[:].bitcast(I32), 0)
         nc.vector.memset(wvol_plane[:].bitcast(I32), 0)
         nc.sync.dma_start(out=wev[:].bitcast(I32), in_=wev_words[0].rearrange("p c i -> p (c i)").bitcast(I32))
@@ -80,101 +148,48 @@ def tile_list_skimming_triage_kernel(
                     out=plane[32 * q : 32 * q + 4, :].bitcast(I32), in_=scales[0, 4 * q : 4 * q + 4, :].bitcast(I32)
                 )
 
-        big = keep.tile([P, 1], F32, name="big")
-        one = keep.tile([P, 1], F32, name="one")
-        nc.vector.memset(big[:], 64.0)
-        nc.scalar.activation(one[:], big[:], ACT.Sigmoid)
-
-        v_words = [
-            keep.tile([P, S], U32, name="v_words0", align_bytes=64),
-            reuse.tile([P, S], U32, name="v_words1", align_bytes=64, offset=8 * T),
-        ]
-        v_planes = keep.tile([P, S], U8, name="v_planes", align_bytes=64)
-        grouped = [
-            [keep.tile([P, PACK, P, PACK], BF16, name=f"grouped0{a}", align_bytes=64) for a in range(PASSES)],
-            [reuse.tile([P, PACK, P, PACK], BF16, name=f"grouped1{a}", align_bytes=64, offset=4 * T + T * a) for a in range(PASSES)],
-        ]
-        w_words = [[keep.tile([P, H], U32, name=f"w_words{c}{a}", align_bytes=64) for a in range(PASSES)] for c in range(2)]
-        w_plane = [[keep.tile([P, H], U8, name=f"w_plane{c}{a}", align_bytes=64) for a in range(PASSES)] for c in range(2)]
-
-        def group_w1(c, a, scalar_share):
-            src = raw[c][a][:].rearrange("p j (m t) -> p m j t", t=PACK)
-            dst = grouped[c][a][:].rearrange("p t m j -> p m j t")
-            if scalar_share:
-                nc.scalar.copy(dst[:, :scalar_share], src[:, :scalar_share])
-            nc.vector.tensor_copy(dst[:, scalar_share:], src[:, scalar_share:])
-
-        def quantize_w1(c, a):
-            flat = grouped[c][a][:].rearrange("p t m j -> p (t m j)")
-            nc.vector.quantize_mx(out=w_words[c][a][:].bitcast(FP8X4), scales=w_plane[c][a][:], in_=flat)
-
-        def stage1_pass(bank, c, a, t, half):
-            rows = slice(t * P, (t + 1) * P)
-            cols = slice(half * BANK, (half + 1) * BANK)
-            nc.tensor.matmul_mx(
-                out=bank[:],
-                lhsT=w_words[c][a][:, rows].bitcast(FP8X4),
-                lhsT_scale=w_plane[c][a][:, rows],
-                rhs=v_words[a][:, cols].bitcast(FP8X4),
-                rhs_scale=v_planes[4 * a :, cols],
-                start=(a == 0),
-                stop=(a == PASSES - 1),
-            )
-
-        h = [[keep.tile([P, S], F32, name=f"h{c}{t}", align_bytes=64) for t in range(PACK)] for c in range(2)]
-        places = [(t, half) for t in range(PACK) for half in range(2)]
-        by_half = [(t, half) for half in range(2) for t in range(PACK)]
-
+        nc.vector.tensor_copy(v_words[1][:], tab[1][:].indirect(offs_sb[:]))
+        group_w1(raw_day1a, DAY, 1, 0, P // 2)
+        group_w1(raw_day1b, DAY, 1, P // 2, 20)
+        quantize_w1(DAY, 1, 2)
+        day_banks = {place: psum.tile([P, BANK], F32, name="bank") for place in places}
         for a in range(PASSES):
-            group_w1(0, a, 64)
-            quantize_w1(0, a)
-        nc.vector.tensor_copy(v_planes[:], tab_planes[:].indirect(offs_sb[:]))
-        nc.vector.tensor_copy(v_words[0][:], tab[0][:].indirect(offs_sb[:]))
-        for half in range(2):
-            nc.vector.tensor_copy(
-                v_words[1][:, half * BANK : (half + 1) * BANK],
-                tab[1][:].indirect(offs_sb[:, half * BANK // 16 : (half + 1) * BANK // 16]),
-            )
-        day_banks = {pl: psum.tile([P, BANK], F32, name="bank") for pl in places}
-        for a in range(PASSES):
-            for t, half in by_half:
-                stage1_pass(day_banks[t, half], 0, a, t, half)
+            for t, half in places:
+                stage1_pass(day_banks[t, half], DAY, a, t, half)
 
-        for a in range(PASSES):
-            group_w1(1, a, 0)
-            quantize_w1(1, a)
+        for a, raw in enumerate((raw_carry0, raw_carry1)):
+            group_w1(raw, CARRY, a, 0, 0)
+            quantize_w1(CARRY, a, 1)
 
         sig = [keep.tile([P, M], F32, name=f"sig{t}", align_bytes=64) for t in range(PACK)]
         th = [keep.tile([P, M], F32, name=f"th{t}", align_bytes=64) for t in range(PACK)]
         diff = [keep.tile([P, M], F32, name=f"diff{t}", align_bytes=64) for t in range(PACK)]
+
         for t in range(PACK):
             for half in range(2):
-                cols = slice(half * BANK, (half + 1) * BANK)
-                if t == 3:
-                    nc.vector.tensor_copy(h[0][t][:, cols], day_banks[t, half][:])
-                else:
-                    nc.scalar.copy(h[0][t][:, cols], day_banks[t, half][:])
-            nc.scalar.activation(sig[t][:], h[0][t][:].indirect(pos1_sb[:]), ACT.Sigmoid, scale=2.0)
+                nc.scalar.copy(h[DAY][t][:, half * BANK : (half + 1) * BANK], day_banks[t, half][:])
+            nc.scalar.activation(sig[t][:], h[DAY][t][:].indirect(pos1_sb[:]), ACT.Sigmoid, scale=2.0)
             nc.vector.tensor_scalar(th[t][:], sig[t][:], 2.0, -1.0, ALU.mult, ALU.add)
-            nc.vector.tensor_tensor(diff[t][:], h[0][t][:].indirect(pos2_sb[:]), th[t][:], ALU.subtract)
+            nc.vector.tensor_tensor(diff[t][:], h[DAY][t][:].indirect(pos2_sb[:]), th[t][:], ALU.subtract)
 
         for t, half in places:
             bank = psum.tile([P, BANK], F32, name="bank")
             for a in range(PASSES):
-                stage1_pass(bank, 1, a, t, half)
-            nc.scalar.copy(h[1][t][:, half * BANK : (half + 1) * BANK], bank[:])
+                stage1_pass(bank, CARRY, a, t, half)
+            nc.scalar.copy(h[CARRY][t][:, half * BANK : (half + 1) * BANK], bank[:])
 
         one_again = keep.tile([P, 1], F32, name="one_again")
-        nc.scalar.activation(one_again[:], sig[PACK - 1][:, 0:1], ACT.Abs_reciprocal_sqrt, scale=0.0, bias=one[:])
+        nc.scalar.activation(one_again[:], h[CARRY][PACK - 1][:, S - 1 : S], ACT.Abs_reciprocal_sqrt, scale=0.0, bias=one[:])
 
-        pairs = BANK // M_PART
-        for part in range(M // M_PART):
+        parts = M // M_PART
+        groups = range(N // P // GROUP)
+        for part in range(parts):
             cases = slice(part * M_PART, (part + 1) * M_PART)
             list_cols = slice(part * M_PART // 16, (part + 1) * M_PART // 16)
-            neg_z = keep.tile([P, PACK, M_PART], F32, name=f"neg_z{part}", align_bytes=64)
+            neg_z = placed(f"neg_z{part}", [P, PACK, M_PART], F32, 56 + 4 * part)
             for t in range(PACK):
-                nc.vector.tensor_tensor(neg_z[:, t, :], h[1][t][:].indirect(pos3_sb[:, list_cols]), diff[t][:, cases], ALU.mult)
-            z_bf = keep.tile([P, M_PART, PACK], BF16, name=f"z_bf{part}", align_bytes=64)
+                nc.vector.tensor_tensor(neg_z[:, t, :], h[CARRY][t][:].indirect(pos3_sb[:, list_cols]), diff[t][:, cases], ALU.mult)
+            z_bf = placed(f"z_bf{part}", [P, M_PART, PACK], BF16, 60 + 4 * part)
             nc.vector.tensor_scalar(
                 z_bf[:].rearrange("p (c i) t -> p c t i", i=4),
                 neg_z[:].rearrange("p t (c i) -> p c t i", i=4),
@@ -183,34 +198,36 @@ def tile_list_skimming_triage_kernel(
             z_words = keep.tile([P, M_PART], U32, name=f"z_words{part}", align_bytes=64)
             z_plane = keep.tile([P, M_PART], U8, name=f"z_plane{part}", align_bytes=64)
             nc.vector.quantize_mx(out=z_words[:].bitcast(FP8X4), scales=z_plane[:], in_=z_bf[:].rearrange("p m t -> p (m t)"))
-            for g in range(N // P // pairs):
-                vol = psum.tile([P, BANK], F32, name="bank")
-                ev = psum.tile([P, BANK], F32, name="bank")
-                for i in range(pairs):
-                    n0 = (g * pairs + i) * P
+            vols = [psum.tile([P, BANK], F32, name="bank") for g in groups]
+            evs = [psum.tile([P, BANK], F32, name="bank") for g in groups]
+            for g in groups:
+                for i in range(GROUP):
+                    n0 = (g * GROUP + i) * P
                     nc.tensor.matmul_mx(
-                        out=vol[:, i * M_PART : (i + 1) * M_PART],
+                        out=vols[g][:, i * M_PART : (i + 1) * M_PART],
                         lhsT=wvol[:, 2 * n0 : 2 * (n0 + P)].bitcast(FP4X4), lhsT_scale=wvol_plane[:, n0 : n0 + P],
                         rhs=z_words[:].bitcast(FP8X4), rhs_scale=z_plane[:], start=True, stop=True,
                     )
-                for i in range(pairs):
-                    n0 = (g * pairs + i) * P
+            for g in groups:
+                for i in range(GROUP):
+                    n0 = (g * GROUP + i) * P
                     nc.tensor.matmul_mx(
-                        out=ev[:, i * M_PART : (i + 1) * M_PART],
+                        out=evs[g][:, i * M_PART : (i + 1) * M_PART],
                         lhsT=wev[:, n0 : n0 + P].bitcast(FP8X4), lhsT_scale=wev_plane[:, n0 : n0 + P],
                         rhs=z_words[:].bitcast(FP8X4), rhs_scale=z_plane[:], start=True, stop=True,
                     )
+            for g in groups:
                 size = ring.tile([P, BANK], F32, name="size")
                 root = ring.tile([P, BANK], F32, name="root")
                 once = ring.tile([P, BANK], F32, name="once")
                 res = ring.tile([P, BANK], F32, name="res")
-                nc.scalar.activation(size[:], vol[:], ACT.Abs)
+                nc.scalar.activation(size[:], vols[g][:], ACT.Abs)
                 nc.scalar.activation(root[:], size[:], ACT.Abs_reciprocal_sqrt, bias=one_again[:])
-                if part == 0:
+                if part < parts - 1:
                     nc.scalar.activation(once[:], root[:], ACT.Square)
-                    nc.vector.tensor_tensor(res[:], ev[:], once[:], ALU.mult)
+                    nc.vector.tensor_tensor(res[:], evs[g][:], once[:], ALU.mult)
                 else:
-                    nc.vector.tensor_tensor(once[:], ev[:], root[:], ALU.mult)
+                    nc.vector.tensor_tensor(once[:], evs[g][:], root[:], ALU.mult)
                     nc.vector.tensor_tensor(res[:], once[:], root[:], ALU.mult)
-                rows = out[g * pairs * P : (g + 1) * pairs * P, cases]
-                nc.sync.dma_start(out=rows.rearrange("(i p) m -> p i m", p=P), in_=res[:].rearrange("p (i m) -> p i m", i=pairs))
+                rows = out[g * GROUP * P : (g + 1) * GROUP * P, cases]
+                nc.sync.dma_start(out=rows.rearrange("(i p) m -> p i m", p=P), in_=res[:].rearrange("p (i m) -> p i m", i=GROUP))

@@ -80,7 +80,7 @@ def tile_list_skimming_triage_kernel(
         nc.sync.dma_start(pos3_sb[:], pos3)
         load_tab(0)
         nc.vector.tensor_copy(v_rows[:], tab_rows[:].indirect(offs_sb[:]))
-        for q in range(4):
+        for q in (0, 2, 1, 3):
             nc.sync.dma_start(
                 out=v_planes[32 * q : 32 * q + 4, :].bitcast(I32), in_=v_rows[8 * q : 8 * q + 8, :].bitcast(I32)
             )
@@ -151,12 +151,13 @@ def tile_list_skimming_triage_kernel(
         nc.vector.tensor_copy(v_words[1][:], tab[1][:].indirect(offs_sb[:]))
         group_w1(raw_day1a, DAY, 1, 0, P // 2)
         group_w1(raw_day1b, DAY, 1, P // 2, 20)
-        quantize_w1(DAY, 1, 2)
+        quantize_w1(DAY, 1, PACK)
         day_banks = {place: psum.tile([P, BANK], F32, name="bank") for place in places}
         for a in range(PASSES):
             for t, half in places:
                 stage1_pass(day_banks[t, half], DAY, a, t, half)
 
+        nc.vector.tensor_copy(h[DAY][0][:, BANK:], day_banks[0, 1][:])
         for a, raw in enumerate((raw_carry0, raw_carry1)):
             group_w1(raw, CARRY, a, 0, 0)
             quantize_w1(CARRY, a, 1)
@@ -167,7 +168,8 @@ def tile_list_skimming_triage_kernel(
 
         for t in range(PACK):
             for half in range(2):
-                nc.scalar.copy(h[DAY][t][:, half * BANK : (half + 1) * BANK], day_banks[t, half][:])
+                if (t, half) != (0, 1):
+                    nc.scalar.copy(h[DAY][t][:, half * BANK : (half + 1) * BANK], day_banks[t, half][:])
             nc.scalar.activation(sig[t][:], h[DAY][t][:].indirect(pos1_sb[:]), ACT.Sigmoid, scale=2.0)
             nc.vector.tensor_scalar(th[t][:], sig[t][:], 2.0, -1.0, ALU.mult, ALU.add)
             nc.vector.tensor_tensor(diff[t][:], h[DAY][t][:].indirect(pos2_sb[:]), th[t][:], ALU.subtract)
@@ -223,11 +225,21 @@ def tile_list_skimming_triage_kernel(
                 res = ring.tile([P, BANK], F32, name="res")
                 nc.scalar.activation(size[:], vols[g][:], ACT.Abs)
                 nc.scalar.activation(root[:], size[:], ACT.Abs_reciprocal_sqrt, bias=one_again[:])
-                if part < parts - 1:
-                    nc.scalar.activation(once[:], root[:], ACT.Square)
-                    nc.vector.tensor_tensor(res[:], evs[g][:], once[:], ALU.mult)
-                else:
-                    nc.vector.tensor_tensor(once[:], evs[g][:], root[:], ALU.mult)
-                    nc.vector.tensor_tensor(res[:], once[:], root[:], ALU.mult)
-                rows = out[g * GROUP * P : (g + 1) * GROUP * P, cases]
-                nc.sync.dma_start(out=rows.rearrange("(i p) m -> p i m", p=P), in_=res[:].rearrange("p (i m) -> p i m", i=GROUP))
+                last_group = g == groups[-1]
+                last_part = part == parts - 1
+                pieces = GROUP if last_group and last_part else 1
+                width = BANK // pieces
+                for i in range(pieces):
+                    cols = slice(i * width, (i + 1) * width)
+                    if last_group == last_part:
+                        nc.scalar.activation(once[:, cols], root[:, cols], ACT.Square)
+                        nc.vector.tensor_tensor(res[:, cols], evs[g][:, cols], once[:, cols], ALU.mult)
+                    else:
+                        nc.vector.tensor_tensor(once[:, cols], evs[g][:, cols], root[:, cols], ALU.mult)
+                        nc.vector.tensor_tensor(res[:, cols], once[:, cols], root[:, cols], ALU.mult)
+                    tiles = GROUP // pieces
+                    first = (g * GROUP + i * tiles) * P
+                    nc.sync.dma_start(
+                        out=out[first : first + tiles * P, cases].rearrange("(i p) m -> p i m", p=P),
+                        in_=res[:, cols].rearrange("p (i m) -> p i m", i=tiles),
+                    )

@@ -92,7 +92,7 @@ def tile_list_skimming_triage_kernel(
         nc.vector.memset(big[:], 64.0)
         nc.scalar.activation(one[:], big[:], ACT.Sigmoid)
 
-        grouped = [[keep.tile([P, PACK, P, PACK], BF16, name=f"grouped{c}{a}", align_bytes=64) for a in range(PASSES)] for c in range(2)]
+        grouped = [[placed(f"grouped{c}{a}", [P, PACK, P, PACK], BF16, 72 + 8 * c + 4 * a) for a in range(PASSES)] for c in range(2)]
         w_words = [[keep.tile([P, H], U32, name=f"w_words{c}{a}", align_bytes=64) for a in range(PASSES)] for c in range(2)]
         w_plane = [[keep.tile([P, H], U8, name=f"w_plane{c}{a}", align_bytes=64) for a in range(PASSES)] for c in range(2)]
 
@@ -162,17 +162,29 @@ def tile_list_skimming_triage_kernel(
             group_w1(raw, CARRY, a, 0, 0)
             quantize_w1(CARRY, a, 1)
 
-        sig = [keep.tile([P, M], F32, name=f"sig{t}", align_bytes=64) for t in range(PACK)]
-        th = [keep.tile([P, M], F32, name=f"th{t}", align_bytes=64) for t in range(PACK)]
-        diff = [keep.tile([P, M], F32, name=f"diff{t}", align_bytes=64) for t in range(PACK)]
+        sig = [
+            [keep.tile([P, M_PART], F32, name=f"sig0{t}", align_bytes=64) for t in range(PACK)],
+            [placed(f"sig1{t}", [P, M_PART], F32, 84 + t) for t in range(PACK)],
+        ]
+        th = [[keep.tile([P, M_PART], F32, name=f"th{part}{t}", align_bytes=64) for t in range(PACK)] for part in range(2)]
+        diff = [[keep.tile([P, M_PART], F32, name=f"diff{part}{t}", align_bytes=64) for t in range(PACK)] for part in range(2)]
+
+        def columns(part):
+            return slice(part * M_PART // 16, (part + 1) * M_PART // 16)
+
+        def squash(part, t):
+            nc.scalar.activation(sig[part][t][:], h[DAY][t][:].indirect(pos1_sb[:, columns(part)]), ACT.Sigmoid, scale=2.0)
+
+        def differ(part, t):
+            nc.vector.tensor_scalar(th[part][t][:], sig[part][t][:], 2.0, -1.0, ALU.mult, ALU.add)
+            nc.vector.tensor_tensor(diff[part][t][:], h[DAY][t][:].indirect(pos2_sb[:, columns(part)]), th[part][t][:], ALU.subtract)
 
         for t in range(PACK):
             for half in range(2):
                 if (t, half) != (0, 1):
                     nc.scalar.copy(h[DAY][t][:, half * BANK : (half + 1) * BANK], day_banks[t, half][:])
-            nc.scalar.activation(sig[t][:], h[DAY][t][:].indirect(pos1_sb[:]), ACT.Sigmoid, scale=2.0)
-            nc.vector.tensor_scalar(th[t][:], sig[t][:], 2.0, -1.0, ALU.mult, ALU.add)
-            nc.vector.tensor_tensor(diff[t][:], h[DAY][t][:].indirect(pos2_sb[:]), th[t][:], ALU.subtract)
+            squash(0, t)
+            differ(0, t)
 
         for t, half in places:
             bank = psum.tile([P, BANK], F32, name="bank")
@@ -180,8 +192,10 @@ def tile_list_skimming_triage_kernel(
                 stage1_pass(bank, CARRY, a, t, half)
             nc.scalar.copy(h[CARRY][t][:, half * BANK : (half + 1) * BANK], bank[:])
 
+        for t in range(PACK):
+            squash(1, t)
         one_again = keep.tile([P, 1], F32, name="one_again")
-        nc.scalar.activation(one_again[:], h[CARRY][PACK - 1][:, S - 1 : S], ACT.Abs_reciprocal_sqrt, scale=0.0, bias=one[:])
+        nc.scalar.activation(one_again[:], sig[1][PACK - 1][:, 0:1], ACT.Abs_reciprocal_sqrt, scale=0.0, bias=one[:])
 
         parts = M // M_PART
         groups = range(N // P // GROUP)
@@ -190,7 +204,7 @@ def tile_list_skimming_triage_kernel(
             list_cols = slice(part * M_PART // 16, (part + 1) * M_PART // 16)
             neg_z = placed(f"neg_z{part}", [P, PACK, M_PART], F32, 56 + 4 * part)
             for t in range(PACK):
-                nc.vector.tensor_tensor(neg_z[:, t, :], h[CARRY][t][:].indirect(pos3_sb[:, list_cols]), diff[t][:, cases], ALU.mult)
+                nc.vector.tensor_tensor(neg_z[:, t, :], h[CARRY][t][:].indirect(pos3_sb[:, list_cols]), diff[part][t][:], ALU.mult)
             z_bf = placed(f"z_bf{part}", [P, M_PART, PACK], BF16, 60 + 4 * part)
             nc.vector.tensor_scalar(
                 z_bf[:].rearrange("p (c i) t -> p c t i", i=4),
@@ -200,6 +214,9 @@ def tile_list_skimming_triage_kernel(
             z_words = keep.tile([P, M_PART], U32, name=f"z_words{part}", align_bytes=64)
             z_plane = keep.tile([P, M_PART], U8, name=f"z_plane{part}", align_bytes=64)
             nc.vector.quantize_mx(out=z_words[:].bitcast(FP8X4), scales=z_plane[:], in_=z_bf[:].rearrange("p m t -> p (m t)"))
+            if part == 0:
+                for t in range(PACK):
+                    differ(1, t)
             vols = [psum.tile([P, BANK], F32, name="bank") for g in groups]
             evs = [psum.tile([P, BANK], F32, name="bank") for g in groups]
             for g in groups:

@@ -46,12 +46,12 @@ def tile_list_skimming_triage_kernel(
             return reuse.tile(shape, dtype, name=name, align_bytes=64, offset=kib * KIB)
 
         tab = [placed("tab0", [P, T], U32, 0), placed("tab1", [P, T], U32, 16)]
-        tab_rows = placed("tab_rows", [P, T], U8, 30)
-        raw_day1a = placed("raw_day1a", [P, PACK, H // 2], F32, 32)
-        raw_carry0 = placed("raw_carry0", [P, PACK, H], F32, 36)
-        raw_day0 = placed("raw_day0", [P, PACK, H], F32, 42)
-        raw_day1b = placed("raw_day1b", [P, PACK, H // 2], F32, 44)
-        raw_carry1 = placed("raw_carry1", [P, PACK, H], F32, 48)
+        tab_rows = placed("tab_rows", [P, T], U8, 32)
+        raw_day1a = placed("raw_day1a", [P, PACK, H // 2], F32, 34)
+        raw_carry0 = placed("raw_carry0", [P, PACK, H], F32, 38)
+        raw_day0 = placed("raw_day0", [P, PACK, H], F32, 44)
+        raw_day1b = placed("raw_day1b", [P, PACK, H // 2], F32, 46)
+        raw_carry1 = placed("raw_carry1", [P, PACK, H], F32, 50)
         wev = placed("wev", [P, N], U32, 0)
         wvol = placed("wvol", [P, 2 * N], U8, 3)
         wev_plane = placed("wev_plane", [P, N], U8, 5)
@@ -79,12 +79,12 @@ def tile_list_skimming_triage_kernel(
         nc.sync.dma_start(pos2_sb[:], pos2)
         nc.sync.dma_start(pos3_sb[:], pos3)
         load_tab(0)
+        load_tab(1)
         nc.vector.tensor_copy(v_rows[:], tab_rows[:].indirect(offs_sb[:]))
         for q in (0, 2, 1, 3):
             nc.sync.dma_start(
                 out=v_planes[32 * q : 32 * q + 4, :].bitcast(I32), in_=v_rows[8 * q : 8 * q + 8, :].bitcast(I32)
             )
-        load_tab(1)
         load_w1(raw_day1a, 1, 0)
 
         big = keep.tile([P, 1], F32, name="big")
@@ -105,6 +105,9 @@ def tile_list_skimming_triage_kernel(
             if scalar_share < count:
                 nc.vector.tensor_copy(dst[:, scalar_share:], src[:, scalar_share:])
 
+        late_words = placed("late_words", [P, P], U32, 46)
+        late_plane = placed("late_plane", [P, P], U8, 47)
+
         def quantize_w1(c, a, calls):
             flat = grouped[c][a][:].rearrange("p t m j -> p (t m j)")
             width = H // calls
@@ -118,10 +121,11 @@ def tile_list_skimming_triage_kernel(
 
         def stage1_pass(bank, c, a, t, half):
             rows = slice(t * P, (t + 1) * P)
+            late = (c, a, t) == (DAY, 0, PACK - 1)
             nc.tensor.matmul_mx(
                 out=bank[:],
-                lhsT=w_words[c][a][:, rows].bitcast(FP8X4),
-                lhsT_scale=w_plane[c][a][:, rows],
+                lhsT=(late_words[:] if late else w_words[c][a][:, rows]).bitcast(FP8X4),
+                lhsT_scale=late_plane[:] if late else w_plane[c][a][:, rows],
                 rhs=v_words[a][:, half * BANK : (half + 1) * BANK].bitcast(FP8X4),
                 rhs_scale=v_planes[:, a * S + half * BANK : a * S + (half + 1) * BANK],
                 start=(a == 0),
@@ -132,7 +136,13 @@ def tile_list_skimming_triage_kernel(
         places = [(t, half) for t in range(PACK) for half in range(2)]
 
         group_w1(raw_day0, DAY, 0, 0, P)
-        quantize_w1(DAY, 0, 1)
+        day0_flat = grouped[DAY][0][:].rearrange("p t m j -> p (t m j)")
+        for first, width in ((0, 2 * P), (2 * P, P)):
+            nc.vector.quantize_mx(
+                out=w_words[DAY][0][:, first : first + width].bitcast(FP8X4),
+                scales=w_plane[DAY][0][:, first : first + width],
+                in_=day0_flat[:, PACK * first : PACK * (first + width)],
+            )
         load_w1(raw_day1b, 1, H // 2)
         load_w1(raw_carry0, 0, H)
         load_w1(raw_carry1, 1, H)
@@ -152,10 +162,14 @@ def tile_list_skimming_triage_kernel(
         group_w1(raw_day1a, DAY, 1, 0, P // 2)
         group_w1(raw_day1b, DAY, 1, P // 2, 20)
         quantize_w1(DAY, 1, PACK)
+        nc.vector.quantize_mx(out=late_words[:].bitcast(FP8X4), scales=late_plane[:], in_=day0_flat[:, PACK * 3 * P :])
         day_banks = {place: psum.tile([P, BANK], F32, name="bank") for place in places}
-        for a in range(PASSES):
-            for t, half in places:
-                stage1_pass(day_banks[t, half], DAY, a, t, half)
+        for t, half in places[:-2]:
+            stage1_pass(day_banks[t, half], DAY, 0, t, half)
+        for t, half in places:
+            if t == PACK - 1:
+                stage1_pass(day_banks[t, half], DAY, 0, t, half)
+            stage1_pass(day_banks[t, half], DAY, 1, t, half)
 
         nc.vector.tensor_copy(h[DAY][0][:, BANK:], day_banks[0, 1][:])
         for a, raw in enumerate((raw_carry0, raw_carry1)):

@@ -190,7 +190,8 @@ def tile_list_skimming_triage_kernel(
             nc.scalar.activation(sig[part][t][:], h[DAY][t][:].indirect(pos1_sb[:, columns(part)]), ACT.Sigmoid, scale=2.0)
 
         def differ(part, t):
-            nc.vector.tensor_scalar(th[part][t][:], sig[part][t][:], 2.0, -1.0, ALU.mult, ALU.add)
+            if part == 0 or t < 2:
+                nc.vector.tensor_scalar(th[part][t][:], sig[part][t][:], 2.0, -1.0, ALU.mult, ALU.add)
             nc.vector.tensor_tensor(diff[part][t][:], h[DAY][t][:].indirect(pos2_sb[:, columns(part)]), th[part][t][:], ALU.subtract)
 
         for t in range(PACK):
@@ -204,10 +205,15 @@ def tile_list_skimming_triage_kernel(
             bank = psum.tile([P, BANK], F32, name="bank")
             for a in range(PASSES):
                 stage1_pass(bank, CARRY, a, t, half)
-            nc.scalar.copy(h[CARRY][t][:, half * BANK : (half + 1) * BANK], bank[:])
+            if (t, half) == places[-1]:
+                nc.vector.tensor_copy(h[CARRY][t][:, half * BANK : (half + 1) * BANK], bank[:])
+            else:
+                nc.scalar.copy(h[CARRY][t][:, half * BANK : (half + 1) * BANK], bank[:])
 
         for t in range(PACK):
             squash(1, t)
+            if t >= 2:
+                nc.scalar.activation(th[1][t][:], sig[1][t][:], ACT.Copy, scale=2.0, bias=-1.0)
         one_again = keep.tile([P, 1], F32, name="one_again")
         nc.scalar.activation(one_again[:], sig[1][PACK - 1][:, 0:1], ACT.Abs_reciprocal_sqrt, scale=0.0, bias=one[:])
 

@@ -226,14 +226,20 @@ def tile_list_skimming_triage_kernel(
             for t in range(PACK):
                 nc.vector.tensor_tensor(neg_z[:, t, :], h[CARRY][t][:].indirect(pos3_sb[:, list_cols]), diff[part][t][:], ALU.mult)
             z_bf = placed(f"z_bf{part}", [P, M_PART, PACK], BF16, 60 + 4 * part)
-            nc.vector.tensor_scalar(
-                z_bf[:].rearrange("p (c i) t -> p c t i", i=4),
-                neg_z[:].rearrange("p t (c i) -> p c t i", i=4),
-                -1.0, None, ALU.mult,
-            )
             z_words = keep.tile([P, M_PART], U32, name=f"z_words{part}", align_bytes=64)
             z_plane = keep.tile([P, M_PART], U8, name=f"z_plane{part}", align_bytes=64)
-            nc.vector.quantize_mx(out=z_words[:].bitcast(FP8X4), scales=z_plane[:], in_=z_bf[:].rearrange("p m t -> p (m t)"))
+            z_pieces = part + 1
+            z_spans = [slice(i * M_PART // z_pieces, (i + 1) * M_PART // z_pieces) for i in range(z_pieces)]
+            for cols in z_spans:
+                nc.vector.tensor_scalar(
+                    z_bf[:, cols, :].rearrange("p (c i) t -> p c t i", i=4),
+                    neg_z[:, :, cols].rearrange("p t (c i) -> p c t i", i=4),
+                    -1.0, None, ALU.mult,
+                )
+            for cols in z_spans:
+                nc.vector.quantize_mx(
+                    out=z_words[:, cols].bitcast(FP8X4), scales=z_plane[:, cols], in_=z_bf[:, cols, :].rearrange("p m t -> p (m t)")
+                )
             if part == 0:
                 for t in range(PACK):
                     differ(1, t)
@@ -261,18 +267,23 @@ def tile_list_skimming_triage_kernel(
                 once = ring.tile([P, BANK], F32, name="once")
                 res = ring.tile([P, BANK], F32, name="res")
                 nc.scalar.activation(size[:], vols[g][:], ACT.Abs)
-                nc.scalar.activation(root[:], size[:], ACT.Abs_reciprocal_sqrt, bias=one_again[:])
                 last_group = g == groups[-1]
                 last_part = part == parts - 1
-                pieces = GROUP if last_group and last_part else 1
+                scalar_squares = last_group == last_part
+                pieces = GROUP if last_part or not scalar_squares else 1
                 width = BANK // pieces
-                for i in range(pieces):
-                    cols = slice(i * width, (i + 1) * width)
-                    if last_group == last_part:
+                spans = [slice(i * width, (i + 1) * width) for i in range(pieces)]
+                for cols in spans if last_part and last_group else [slice(0, BANK)]:
+                    nc.scalar.activation(root[:, cols], size[:, cols], ACT.Abs_reciprocal_sqrt, bias=one_again[:])
+                for cols in spans:
+                    if scalar_squares:
                         nc.scalar.activation(once[:, cols], root[:, cols], ACT.Square)
-                        nc.vector.tensor_tensor(res[:, cols], evs[g][:, cols], once[:, cols], ALU.mult)
                     else:
                         nc.vector.tensor_tensor(once[:, cols], evs[g][:, cols], root[:, cols], ALU.mult)
+                for i, cols in enumerate(spans):
+                    if scalar_squares:
+                        nc.vector.tensor_tensor(res[:, cols], evs[g][:, cols], once[:, cols], ALU.mult)
+                    else:
                         nc.vector.tensor_tensor(res[:, cols], once[:, cols], root[:, cols], ALU.mult)
                     tiles = GROUP // pieces
                     first = (g * GROUP + i * tiles) * P

@@ -20,10 +20,18 @@ P = 128
 PACK = 4
 PASSES = K // (P * PACK)
 BANK = 512
-M_PART = 256
-GROUP = BANK // M_PART
+QUADRANT = 32
+LIST_ROWS = 16
 KIB = 1024
 DAY, CARRY = 0, 1
+
+M_PART = 256
+PARTS = M // M_PART
+GROUP = BANK // M_PART
+
+LAST_SCALAR_SHARE = 20
+FIRST_SCALAR_TANH = 2
+SATURATED = 64.0
 
 
 def tile_list_skimming_triage_kernel(
@@ -37,10 +45,10 @@ def tile_list_skimming_triage_kernel(
         ring = ctx.enter_context(tc.tile_pool(name="ring", bufs=4))
         psum = ctx.enter_context(tc.psum_pool(name="psum", bufs=8))
 
-        offs_sb = lists.tile([P, S // 16], U16, name="offs_sb")
-        pos1_sb = lists.tile([P, M // 16], U16, name="pos1_sb")
-        pos2_sb = lists.tile([P, M // 16], U16, name="pos2_sb")
-        pos3_sb = lists.tile([P, M // 16], U16, name="pos3_sb")
+        offs_sb = lists.tile([P, S // LIST_ROWS], U16, name="offs_sb")
+        pos1_sb = lists.tile([P, M // LIST_ROWS], U16, name="pos1_sb")
+        pos2_sb = lists.tile([P, M // LIST_ROWS], U16, name="pos2_sb")
+        pos3_sb = lists.tile([P, M // LIST_ROWS], U16, name="pos3_sb")
 
         def placed(name, shape, dtype, kib):
             return reuse.tile(shape, dtype, name=name, align_bytes=64, offset=kib * KIB)
@@ -68,12 +76,12 @@ def tile_list_skimming_triage_kernel(
         v_rows = keep.tile([P, S], U8, name="v_rows", align_bytes=64)
         v_planes = keep.tile([P, PASSES * S], U8, name="v_planes", align_bytes=64)
 
-        nc.vector.memset(tab_rows[32:64, :].bitcast(I32), 0)
-        nc.vector.memset(tab_rows[64:128, :].bitcast(I32), 0)
+        nc.vector.memset(tab_rows[QUADRANT : 2 * QUADRANT, :].bitcast(I32), 0)
+        nc.vector.memset(tab_rows[2 * QUADRANT :, :].bitcast(I32), 0)
         nc.vector.memset(v_planes[:].bitcast(I32), 0)
         nc.sync.dma_start(offs_sb[:], offs)
         for a in range(PASSES):
-            nc.sync.dma_start(out=tab_rows[a:32:PASSES, :].bitcast(I32), in_=tab_scales[a].bitcast(I32))
+            nc.sync.dma_start(out=tab_rows[a:QUADRANT:PASSES, :].bitcast(I32), in_=tab_scales[a].bitcast(I32))
         load_w1(raw_day0, 0, 0)
         nc.sync.dma_start(pos1_sb[:], pos1)
         nc.sync.dma_start(pos2_sb[:], pos2)
@@ -81,15 +89,17 @@ def tile_list_skimming_triage_kernel(
         load_tab(0)
         load_tab(1)
         nc.vector.tensor_copy(v_rows[:], tab_rows[:].indirect(offs_sb[:]))
+        rows_per_move = PACK * PASSES
         for q in (0, 2, 1, 3):
             nc.sync.dma_start(
-                out=v_planes[32 * q : 32 * q + 4, :].bitcast(I32), in_=v_rows[8 * q : 8 * q + 8, :].bitcast(I32)
+                out=v_planes[QUADRANT * q : QUADRANT * q + PACK, :].bitcast(I32),
+                in_=v_rows[rows_per_move * q : rows_per_move * (q + 1), :].bitcast(I32),
             )
         load_w1(raw_day1a, 1, 0)
 
         big = keep.tile([P, 1], F32, name="big")
         one = keep.tile([P, 1], F32, name="one")
-        nc.vector.memset(big[:], 64.0)
+        nc.vector.memset(big[:], SATURATED)
         nc.scalar.activation(one[:], big[:], ACT.Sigmoid)
 
         grouped = [[placed(f"grouped{c}{a}", [P, PACK, P, PACK], BF16, 72 + 8 * c + 4 * a) for a in range(PASSES)] for c in range(2)]
@@ -153,16 +163,17 @@ def tile_list_skimming_triage_kernel(
         nc.sync.dma_start(out=wev[:].bitcast(I32), in_=wev_words[0].rearrange("p c i -> p (c i)").bitcast(I32))
         nc.sync.dma_start(out=wvol[:].bitcast(I32), in_=wvol_words[0].bitcast(I32))
         for plane, scales in ((wev_plane, wev_scales), (wvol_plane, wvol_scales)):
-            for q in range(4):
+            for q in range(P // QUADRANT):
                 nc.sync.dma_start(
-                    out=plane[32 * q : 32 * q + 4, :].bitcast(I32), in_=scales[0, 4 * q : 4 * q + 4, :].bitcast(I32)
+                    out=plane[QUADRANT * q : QUADRANT * q + PACK, :].bitcast(I32),
+                    in_=scales[0, PACK * q : PACK * (q + 1), :].bitcast(I32),
                 )
 
         nc.vector.tensor_copy(v_words[1][:], tab[1][:].indirect(offs_sb[:]))
         group_w1(raw_day1a, DAY, 1, 0, P // 2)
-        group_w1(raw_day1b, DAY, 1, P // 2, 20)
+        group_w1(raw_day1b, DAY, 1, P // 2, LAST_SCALAR_SHARE)
         quantize_w1(DAY, 1, PACK)
-        nc.vector.quantize_mx(out=late_words[:].bitcast(FP8X4), scales=late_plane[:], in_=day0_flat[:, PACK * 3 * P :])
+        nc.vector.quantize_mx(out=late_words[:].bitcast(FP8X4), scales=late_plane[:], in_=day0_flat[:, PACK * (PACK - 1) * P :])
         day_banks = {place: psum.tile([P, BANK], F32, name="bank") for place in places}
         for t, half in places[:-2]:
             stage1_pass(day_banks[t, half], DAY, 0, t, half)
@@ -180,17 +191,17 @@ def tile_list_skimming_triage_kernel(
             [keep.tile([P, M_PART], F32, name=f"sig0{t}", align_bytes=64) for t in range(PACK)],
             [placed(f"sig1{t}", [P, M_PART], F32, 84 + t) for t in range(PACK)],
         ]
-        th = [[keep.tile([P, M_PART], F32, name=f"th{part}{t}", align_bytes=64) for t in range(PACK)] for part in range(2)]
-        diff = [[keep.tile([P, M_PART], F32, name=f"diff{part}{t}", align_bytes=64) for t in range(PACK)] for part in range(2)]
+        th = [[keep.tile([P, M_PART], F32, name=f"th{part}{t}", align_bytes=64) for t in range(PACK)] for part in range(PARTS)]
+        diff = [[keep.tile([P, M_PART], F32, name=f"diff{part}{t}", align_bytes=64) for t in range(PACK)] for part in range(PARTS)]
 
         def columns(part):
-            return slice(part * M_PART // 16, (part + 1) * M_PART // 16)
+            return slice(part * M_PART // LIST_ROWS, (part + 1) * M_PART // LIST_ROWS)
 
         def squash(part, t):
             nc.scalar.activation(sig[part][t][:], h[DAY][t][:].indirect(pos1_sb[:, columns(part)]), ACT.Sigmoid, scale=2.0)
 
         def differ(part, t):
-            if part == 0 or t < 2:
+            if part == 0 or t < FIRST_SCALAR_TANH:
                 nc.vector.tensor_scalar(th[part][t][:], sig[part][t][:], 2.0, -1.0, ALU.mult, ALU.add)
             nc.vector.tensor_tensor(diff[part][t][:], h[DAY][t][:].indirect(pos2_sb[:, columns(part)]), th[part][t][:], ALU.subtract)
 
@@ -212,37 +223,36 @@ def tile_list_skimming_triage_kernel(
 
         for t in range(PACK):
             squash(1, t)
-            if t >= 2:
+            if t >= FIRST_SCALAR_TANH:
                 nc.scalar.activation(th[1][t][:], sig[1][t][:], ACT.Copy, scale=2.0, bias=-1.0)
-        one_again = keep.tile([P, 1], F32, name="one_again")
-        nc.scalar.activation(one_again[:], sig[1][PACK - 1][:, 0:1], ACT.Abs_reciprocal_sqrt, scale=0.0, bias=one[:])
+        one_again = placed("one_again", [P, 1], F32, 84 + PACK - 1)
+        nc.scalar.activation(one_again[:], one[:], ACT.Abs_reciprocal_sqrt)
 
-        parts = M // M_PART
         groups = range(N // P // GROUP)
-        for part in range(parts):
+        for part in range(PARTS):
+            last_part = part == PARTS - 1
             cases = slice(part * M_PART, (part + 1) * M_PART)
-            list_cols = slice(part * M_PART // 16, (part + 1) * M_PART // 16)
             neg_z = placed(f"neg_z{part}", [P, PACK, M_PART], F32, 56 + 4 * part)
             for t in range(PACK):
-                nc.vector.tensor_tensor(neg_z[:, t, :], h[CARRY][t][:].indirect(pos3_sb[:, list_cols]), diff[part][t][:], ALU.mult)
+                nc.vector.tensor_tensor(neg_z[:, t, :], h[CARRY][t][:].indirect(pos3_sb[:, columns(part)]), diff[part][t][:], ALU.mult)
             z_bf = placed(f"z_bf{part}", [P, M_PART, PACK], BF16, 60 + 4 * part)
             z_words = keep.tile([P, M_PART], U32, name=f"z_words{part}", align_bytes=64)
             z_plane = keep.tile([P, M_PART], U8, name=f"z_plane{part}", align_bytes=64)
-            z_pieces = part + 1
+            z_pieces = 2 if last_part else 1
             z_spans = [slice(i * M_PART // z_pieces, (i + 1) * M_PART // z_pieces) for i in range(z_pieces)]
             for cols in z_spans:
                 nc.vector.tensor_scalar(
-                    z_bf[:, cols, :].rearrange("p (c i) t -> p c t i", i=4),
-                    neg_z[:, :, cols].rearrange("p t (c i) -> p c t i", i=4),
+                    z_bf[:, cols, :].rearrange("p (c i) t -> p c t i", i=PACK),
+                    neg_z[:, :, cols].rearrange("p t (c i) -> p c t i", i=PACK),
                     -1.0, None, ALU.mult,
                 )
             for cols in z_spans:
                 nc.vector.quantize_mx(
                     out=z_words[:, cols].bitcast(FP8X4), scales=z_plane[:, cols], in_=z_bf[:, cols, :].rearrange("p m t -> p (m t)")
                 )
-            if part == 0:
+            if not last_part:
                 for t in range(PACK):
-                    differ(1, t)
+                    differ(part + 1, t)
             vols = [psum.tile([P, BANK], F32, name="bank") for g in groups]
             evs = [psum.tile([P, BANK], F32, name="bank") for g in groups]
             for g in groups:
@@ -264,11 +274,10 @@ def tile_list_skimming_triage_kernel(
             for g in groups:
                 size = ring.tile([P, BANK], F32, name="size")
                 root = ring.tile([P, BANK], F32, name="root")
-                once = ring.tile([P, BANK], F32, name="once")
+                between = ring.tile([P, BANK], F32, name="between")
                 res = ring.tile([P, BANK], F32, name="res")
                 nc.scalar.activation(size[:], vols[g][:], ACT.Abs)
                 last_group = g == groups[-1]
-                last_part = part == parts - 1
                 scalar_squares = last_group == last_part
                 pieces = GROUP if last_part or not scalar_squares else 1
                 width = BANK // pieces
@@ -277,14 +286,14 @@ def tile_list_skimming_triage_kernel(
                     nc.scalar.activation(root[:, cols], size[:, cols], ACT.Abs_reciprocal_sqrt, bias=one_again[:])
                 for cols in spans:
                     if scalar_squares:
-                        nc.scalar.activation(once[:, cols], root[:, cols], ACT.Square)
+                        nc.scalar.activation(between[:, cols], root[:, cols], ACT.Square)
                     else:
-                        nc.vector.tensor_tensor(once[:, cols], evs[g][:, cols], root[:, cols], ALU.mult)
+                        nc.vector.tensor_tensor(between[:, cols], evs[g][:, cols], root[:, cols], ALU.mult)
                 for i, cols in enumerate(spans):
                     if scalar_squares:
-                        nc.vector.tensor_tensor(res[:, cols], evs[g][:, cols], once[:, cols], ALU.mult)
+                        nc.vector.tensor_tensor(res[:, cols], evs[g][:, cols], between[:, cols], ALU.mult)
                     else:
-                        nc.vector.tensor_tensor(res[:, cols], once[:, cols], root[:, cols], ALU.mult)
+                        nc.vector.tensor_tensor(res[:, cols], between[:, cols], root[:, cols], ALU.mult)
                     tiles = GROUP // pieces
                     first = (g * GROUP + i * tiles) * P
                     nc.sync.dma_start(

@@ -30,7 +30,8 @@ PARTS = M // M_PART
 GROUP = BANK // M_PART
 
 LAST_SCALAR_SHARE = 20
-FIRST_SCALAR_TANH = 2
+VECTOR_DAY_BANKS = ((0, 1),)
+VECTOR_CARRY_BANKS = ((1, 1), (3, 1))
 SATURATED = 64.0
 
 
@@ -53,17 +54,17 @@ def tile_list_skimming_triage_kernel(
         def placed(name, shape, dtype, kib):
             return reuse.tile(shape, dtype, name=name, align_bytes=64, offset=kib * KIB)
 
-        tab = [placed("tab0", [P, T], U32, 0), placed("tab1", [P, T], U32, 16)]
-        tab_rows = placed("tab_rows", [P, T], U8, 32)
-        raw_day1a = placed("raw_day1a", [P, PACK, H // 2], F32, 34)
-        raw_carry0 = placed("raw_carry0", [P, PACK, H], F32, 38)
-        raw_day0 = placed("raw_day0", [P, PACK, H], F32, 44)
-        raw_day1b = placed("raw_day1b", [P, PACK, H // 2], F32, 46)
-        raw_carry1 = placed("raw_carry1", [P, PACK, H], F32, 50)
-        wev = placed("wev", [P, N], U32, 0)
-        wvol = placed("wvol", [P, 2 * N], U8, 3)
-        wev_plane = placed("wev_plane", [P, N], U8, 5)
-        wvol_plane = placed("wvol_plane", [P, N], U8, 6)
+        tab = [placed("tab0", [P, T], U32, 0), placed("tab1", [P, T], U32, 20)]
+        staging = placed("staging", [P, 54 * KIB], U8, 16)
+        raw_day0 = placed("raw_day0", [P, PACK, H], F32, 108)
+        raw_day1a = placed("raw_day1a", [P, PACK, H // 2], F32, 36)
+        raw_day1b = placed("raw_day1b", [P, PACK, H // 2], F32, 40)
+        raw_carry0 = placed("raw_carry0", [P, PACK, H], F32, 46)
+        raw_carry1 = placed("raw_carry1", [P, PACK, H], F32, 54)
+        wev = placed("wev", [P, N], U32, 62)
+        wvol = placed("wvol", [P, 2 * N], U8, 65)
+        wev_plane = placed("wev_plane", [P, N], U8, 67)
+        wvol_plane = placed("wvol_plane", [P, N], U8, 68)
 
         def load_w1(raw, a, first):
             rows = w1[a * P * PACK : (a + 1) * P * PACK, first : first + raw.shape[2]]
@@ -72,29 +73,31 @@ def tile_list_skimming_triage_kernel(
         def load_tab(a):
             nc.sync.dma_start(out=tab[a][:].bitcast(I32), in_=tab_words[a].rearrange("p t i -> p (t i)").bitcast(I32))
 
-        v_words = [keep.tile([P, S], U32, name=f"v_words{a}", align_bytes=64) for a in range(PASSES)]
+        v_words = [placed(f"v_words{a}", [P, S], U32, 104 - 4 * a) for a in range(PASSES)]
         v_rows = keep.tile([P, S], U8, name="v_rows", align_bytes=64)
-        v_planes = keep.tile([P, PASSES * S], U8, name="v_planes", align_bytes=64)
+        v_planes = [keep.tile([P, S], U8, name="v_plane0", align_bytes=64), placed("v_plane1", [P, S], U8, 44)]
 
-        nc.vector.memset(tab_rows[QUADRANT : 2 * QUADRANT, :].bitcast(I32), 0)
-        nc.vector.memset(tab_rows[2 * QUADRANT :, :].bitcast(I32), 0)
-        nc.vector.memset(v_planes[:].bitcast(I32), 0)
+        nc.vector.memset(staging[QUADRANT : 2 * QUADRANT, :T].bitcast(I32), 0)
+        nc.vector.memset(staging[2 * QUADRANT :, :T].bitcast(I32), 0)
         nc.sync.dma_start(offs_sb[:], offs)
-        for a in range(PASSES):
-            nc.sync.dma_start(out=tab_rows[a:QUADRANT:PASSES, :].bitcast(I32), in_=tab_scales[a].bitcast(I32))
+        nc.sync.dma_start(out=staging[:QUADRANT, :T].bitcast(I32), in_=tab_scales.rearrange("a q t -> (a q) t").bitcast(I32))
         load_w1(raw_day0, 0, 0)
         nc.sync.dma_start(pos1_sb[:], pos1)
         nc.sync.dma_start(pos2_sb[:], pos2)
         nc.sync.dma_start(pos3_sb[:], pos3)
         load_tab(0)
+        nc.vector.tensor_copy(v_rows[:], staging[:, :T].indirect(offs_sb[:]))
+        rows_per_pass = QUADRANT // PASSES
+
+        def move_scales(a):
+            for i in range(PACK):
+                nc.sync.dma_start(
+                    out=v_planes[a][PACK * a + i :: QUADRANT, :].bitcast(I32),
+                    in_=v_rows[rows_per_pass * a + i : rows_per_pass * (a + 1) : PACK, :].bitcast(I32),
+                )
+
+        move_scales(0)
         load_tab(1)
-        nc.vector.tensor_copy(v_rows[:], tab_rows[:].indirect(offs_sb[:]))
-        rows_per_move = PACK * PASSES
-        for q in (0, 2, 1, 3):
-            nc.sync.dma_start(
-                out=v_planes[QUADRANT * q : QUADRANT * q + PACK, :].bitcast(I32),
-                in_=v_rows[rows_per_move * q : rows_per_move * (q + 1), :].bitcast(I32),
-            )
         load_w1(raw_day1a, 1, 0)
 
         big = keep.tile([P, 1], F32, name="big")
@@ -115,9 +118,6 @@ def tile_list_skimming_triage_kernel(
             if scalar_share < count:
                 nc.vector.tensor_copy(dst[:, scalar_share:], src[:, scalar_share:])
 
-        late_words = placed("late_words", [P, P], U32, 46)
-        late_plane = placed("late_plane", [P, P], U8, 47)
-
         def quantize_w1(c, a, calls):
             flat = grouped[c][a][:].rearrange("p t m j -> p (t m j)")
             width = H // calls
@@ -131,13 +131,12 @@ def tile_list_skimming_triage_kernel(
 
         def stage1_pass(bank, c, a, t, half):
             rows = slice(t * P, (t + 1) * P)
-            late = (c, a, t) == (DAY, 0, PACK - 1)
             nc.tensor.matmul_mx(
                 out=bank[:],
-                lhsT=(late_words[:] if late else w_words[c][a][:, rows]).bitcast(FP8X4),
-                lhsT_scale=late_plane[:] if late else w_plane[c][a][:, rows],
+                lhsT=w_words[c][a][:, rows].bitcast(FP8X4),
+                lhsT_scale=w_plane[c][a][:, rows],
                 rhs=v_words[a][:, half * BANK : (half + 1) * BANK].bitcast(FP8X4),
-                rhs_scale=v_planes[:, a * S + half * BANK : a * S + (half + 1) * BANK],
+                rhs_scale=v_planes[a][PACK * a :, half * BANK : (half + 1) * BANK],
                 start=(a == 0),
                 stop=(a == PASSES - 1),
             )
@@ -146,20 +145,14 @@ def tile_list_skimming_triage_kernel(
         places = [(t, half) for t in range(PACK) for half in range(2)]
 
         group_w1(raw_day0, DAY, 0, 0, P)
-        day0_flat = grouped[DAY][0][:].rearrange("p t m j -> p (t m j)")
-        for first, width in ((0, 2 * P), (2 * P, P)):
-            nc.vector.quantize_mx(
-                out=w_words[DAY][0][:, first : first + width].bitcast(FP8X4),
-                scales=w_plane[DAY][0][:, first : first + width],
-                in_=day0_flat[:, PACK * first : PACK * (first + width)],
-            )
+        quantize_w1(DAY, 0, 1)
         load_w1(raw_day1b, 1, H // 2)
+        move_scales(1)
+        nc.vector.tensor_copy(v_words[0][:], tab[0][:].indirect(offs_sb[:]))
         load_w1(raw_carry0, 0, H)
         load_w1(raw_carry1, 1, H)
-        nc.vector.tensor_copy(v_words[0][:], tab[0][:].indirect(offs_sb[:]))
 
-        nc.vector.memset(wev_plane[:].bitcast(I32), 0)
-        nc.vector.memset(wvol_plane[:].bitcast(I32), 0)
+        nc.vector.tensor_copy(v_words[1][:], tab[1][:].indirect(offs_sb[:]))
         nc.sync.dma_start(out=wev[:].bitcast(I32), in_=wev_words[0].rearrange("p c i -> p (c i)").bitcast(I32))
         nc.sync.dma_start(out=wvol[:].bitcast(I32), in_=wvol_words[0].bitcast(I32))
         for plane, scales in ((wev_plane, wev_scales), (wvol_plane, wvol_scales)):
@@ -169,20 +162,27 @@ def tile_list_skimming_triage_kernel(
                     in_=scales[0, PACK * q : PACK * (q + 1), :].bitcast(I32),
                 )
 
-        nc.vector.tensor_copy(v_words[1][:], tab[1][:].indirect(offs_sb[:]))
         group_w1(raw_day1a, DAY, 1, 0, P // 2)
         group_w1(raw_day1b, DAY, 1, P // 2, LAST_SCALAR_SHARE)
         quantize_w1(DAY, 1, PACK)
-        nc.vector.quantize_mx(out=late_words[:].bitcast(FP8X4), scales=late_plane[:], in_=day0_flat[:, PACK * (PACK - 1) * P :])
         day_banks = {place: psum.tile([P, BANK], F32, name="bank") for place in places}
-        for t, half in places[:-2]:
-            stage1_pass(day_banks[t, half], DAY, 0, t, half)
-        for t, half in places:
-            if t == PACK - 1:
-                stage1_pass(day_banks[t, half], DAY, 0, t, half)
-            stage1_pass(day_banks[t, half], DAY, 1, t, half)
+        for a in range(PASSES):
+            for t, half in places:
+                stage1_pass(day_banks[t, half], DAY, a, t, half)
 
-        nc.vector.tensor_copy(h[DAY][0][:, BANK:], day_banks[0, 1][:])
+        def empty(c, t, half, bank, on_vector):
+            dst = h[c][t][:, half * BANK : (half + 1) * BANK]
+            if c == DAY and on_vector:
+                nc.vector.tensor_scalar(dst, bank[:], 0.5, 0.5, ALU.mult, ALU.add)
+            elif c == DAY:
+                nc.scalar.activation(dst, bank[:], ACT.Copy, scale=0.5, bias=0.5)
+            elif on_vector:
+                nc.vector.tensor_copy(dst, bank[:])
+            else:
+                nc.scalar.copy(dst, bank[:])
+
+        for t, half in VECTOR_DAY_BANKS:
+            empty(DAY, t, half, day_banks[t, half], True)
         for a, raw in enumerate((raw_carry0, raw_carry1)):
             group_w1(raw, CARRY, a, 0, 0)
             quantize_w1(CARRY, a, 1)
@@ -191,24 +191,24 @@ def tile_list_skimming_triage_kernel(
             [keep.tile([P, M_PART], F32, name=f"sig0{t}", align_bytes=64) for t in range(PACK)],
             [placed(f"sig1{t}", [P, M_PART], F32, 84 + t) for t in range(PACK)],
         ]
-        th = [[keep.tile([P, M_PART], F32, name=f"th{part}{t}", align_bytes=64) for t in range(PACK)] for part in range(PARTS)]
-        diff = [[keep.tile([P, M_PART], F32, name=f"diff{part}{t}", align_bytes=64) for t in range(PACK)] for part in range(PARTS)]
+        diff = [
+            [placed(f"diff0{t}", [P, M_PART], F32, 46 if t == 0 else 54 + t) for t in range(PACK)],
+            [keep.tile([P, M_PART], F32, name=f"diff1{t}", align_bytes=64) for t in range(PACK)],
+        ]
 
         def columns(part):
             return slice(part * M_PART // LIST_ROWS, (part + 1) * M_PART // LIST_ROWS)
 
         def squash(part, t):
-            nc.scalar.activation(sig[part][t][:], h[DAY][t][:].indirect(pos1_sb[:, columns(part)]), ACT.Sigmoid, scale=2.0)
+            nc.scalar.activation(sig[part][t][:], h[DAY][t][:].indirect(pos1_sb[:, columns(part)]), ACT.Sigmoid, scale=4.0, bias=-2.0)
 
         def differ(part, t):
-            if part == 0 or t < FIRST_SCALAR_TANH:
-                nc.vector.tensor_scalar(th[part][t][:], sig[part][t][:], 2.0, -1.0, ALU.mult, ALU.add)
-            nc.vector.tensor_tensor(diff[part][t][:], h[DAY][t][:].indirect(pos2_sb[:, columns(part)]), th[part][t][:], ALU.subtract)
+            nc.vector.tensor_tensor(diff[part][t][:], h[DAY][t][:].indirect(pos2_sb[:, columns(part)]), sig[part][t][:], ALU.subtract)
 
         for t in range(PACK):
             for half in range(2):
-                if (t, half) != (0, 1):
-                    nc.scalar.copy(h[DAY][t][:, half * BANK : (half + 1) * BANK], day_banks[t, half][:])
+                if (t, half) not in VECTOR_DAY_BANKS:
+                    empty(DAY, t, half, day_banks[t, half], False)
             squash(0, t)
             differ(0, t)
 
@@ -216,26 +216,21 @@ def tile_list_skimming_triage_kernel(
             bank = psum.tile([P, BANK], F32, name="bank")
             for a in range(PASSES):
                 stage1_pass(bank, CARRY, a, t, half)
-            if (t, half) == places[-1]:
-                nc.vector.tensor_copy(h[CARRY][t][:, half * BANK : (half + 1) * BANK], bank[:])
-            else:
-                nc.scalar.copy(h[CARRY][t][:, half * BANK : (half + 1) * BANK], bank[:])
+            empty(CARRY, t, half, bank, (t, half) in VECTOR_CARRY_BANKS)
 
         for t in range(PACK):
             squash(1, t)
-            if t >= FIRST_SCALAR_TANH:
-                nc.scalar.activation(th[1][t][:], sig[1][t][:], ACT.Copy, scale=2.0, bias=-1.0)
-        one_again = placed("one_again", [P, 1], F32, 84 + PACK - 1)
+        one_again = placed("one_again", [P, 1], F32, 100)
         nc.scalar.activation(one_again[:], one[:], ACT.Abs_reciprocal_sqrt)
 
         groups = range(N // P // GROUP)
         for part in range(PARTS):
             last_part = part == PARTS - 1
             cases = slice(part * M_PART, (part + 1) * M_PART)
-            neg_z = placed(f"neg_z{part}", [P, PACK, M_PART], F32, 56 + 4 * part)
+            neg_z = placed(f"neg_z{part}", [P, PACK, M_PART], F32, 116 + 4 * part)
             for t in range(PACK):
                 nc.vector.tensor_tensor(neg_z[:, t, :], h[CARRY][t][:].indirect(pos3_sb[:, columns(part)]), diff[part][t][:], ALU.mult)
-            z_bf = placed(f"z_bf{part}", [P, M_PART, PACK], BF16, 60 + 4 * part)
+            z_bf = placed(f"z_bf{part}", [P, M_PART, PACK], BF16, 120 + 4 * part)
             z_words = keep.tile([P, M_PART], U32, name=f"z_words{part}", align_bytes=64)
             z_plane = keep.tile([P, M_PART], U8, name=f"z_plane{part}", align_bytes=64)
             z_pieces = 2 if last_part else 1
@@ -244,7 +239,7 @@ def tile_list_skimming_triage_kernel(
                 nc.vector.tensor_scalar(
                     z_bf[:, cols, :].rearrange("p (c i) t -> p c t i", i=PACK),
                     neg_z[:, :, cols].rearrange("p t (c i) -> p c t i", i=PACK),
-                    -1.0, None, ALU.mult,
+                    -2.0, None, ALU.mult,
                 )
             for cols in z_spans:
                 nc.vector.quantize_mx(

@@ -52,7 +52,7 @@ def tile_list_skimming_triage_kernel(
         pos3_sb = lists.tile([P, M // LIST_ROWS], U16, name="pos3_sb")
 
         def placed(name, shape, dtype, kib):
-            return reuse.tile(shape, dtype, name=name, align_bytes=64, offset=kib * KIB)
+            return reuse.tile(shape, dtype, name=name, align_bytes=64, offset=int(kib * KIB))
 
         tab = [placed("tab0", [P, T], U32, 0), placed("tab1", [P, T], U32, 20)]
         staging = placed("staging", [P, 54 * KIB], U8, 16)
@@ -98,6 +98,7 @@ def tile_list_skimming_triage_kernel(
 
         move_scales(0)
         load_tab(1)
+        move_scales(1)
         load_w1(raw_day1a, 1, 0)
 
         big = keep.tile([P, 1], F32, name="big")
@@ -147,7 +148,6 @@ def tile_list_skimming_triage_kernel(
         group_w1(raw_day0, DAY, 0, 0, P)
         quantize_w1(DAY, 0, 1)
         load_w1(raw_day1b, 1, H // 2)
-        move_scales(1)
         nc.vector.tensor_copy(v_words[0][:], tab[0][:].indirect(offs_sb[:]))
         load_w1(raw_carry0, 0, H)
         load_w1(raw_carry1, 1, H)

@@ -107,7 +107,10 @@ def tile_list_skimming_triage_kernel(
         nc.scalar.activation(one[:], big[:], ACT.Sigmoid)
 
         grouped = [[placed(f"grouped{c}{a}", [P, PACK, P, PACK], BF16, 72 + 8 * c + 4 * a) for a in range(PASSES)] for c in range(2)]
-        w_words = [[keep.tile([P, H], U32, name=f"w_words{c}{a}", align_bytes=64) for a in range(PASSES)] for c in range(2)]
+        w_words = [
+            [placed("w_words00", [P, H], U32, 0) if (c, a) == (DAY, 0) else keep.tile([P, H], U32, name=f"w_words{c}{a}", align_bytes=64) for a in range(PASSES)]
+            for c in range(2)
+        ]
         w_plane = [[keep.tile([P, H], U8, name=f"w_plane{c}{a}", align_bytes=64) for a in range(PASSES)] for c in range(2)]
 
         def group_w1(raw, c, a, first, scalar_share):
@@ -146,9 +149,9 @@ def tile_list_skimming_triage_kernel(
         places = [(t, half) for t in range(PACK) for half in range(2)]
 
         group_w1(raw_day0, DAY, 0, 0, P)
-        quantize_w1(DAY, 0, 1)
         load_w1(raw_day1b, 1, H // 2)
         nc.vector.tensor_copy(v_words[0][:], tab[0][:].indirect(offs_sb[:]))
+        quantize_w1(DAY, 0, 1)
         load_w1(raw_carry0, 0, H)
         load_w1(raw_carry1, 1, H)
 

@@ -29,10 +29,14 @@ M_PART = 256
 PARTS = M // M_PART
 GROUP = BANK // M_PART
 
-LAST_SCALAR_SHARE = 20
-VECTOR_DAY_BANKS = ((0, 1),)
-VECTOR_CARRY_BANKS = ((1, 1), (3, 1))
+HALF = P // 2
+CHUNKS = 2
+CHUNK = H // CHUNKS
 SATURATED = 64.0
+C01_SCALAR = 64
+C10_SCALAR = 40
+VECTOR_CARRY_BANKS = ((0, 1, 0), (0, 1, 1))
+VECTOR_DAY_BANKS = ((0, 0), (0, 1), (1, 0), (1, 1), (2, 0), (2, 1), (3, 1))
 
 
 def tile_list_skimming_triage_kernel(
@@ -54,17 +58,14 @@ def tile_list_skimming_triage_kernel(
         def placed(name, shape, dtype, kib):
             return reuse.tile(shape, dtype, name=name, align_bytes=64, offset=int(kib * KIB))
 
-        tab = [placed("tab0", [P, T], U32, 0), placed("tab1", [P, T], U32, 20)]
-        staging = placed("staging", [P, 54 * KIB], U8, 16)
-        raw_day0 = placed("raw_day0", [P, PACK, H], F32, 108)
-        raw_day1a = placed("raw_day1a", [P, PACK, H // 2], F32, 36)
-        raw_day1b = placed("raw_day1b", [P, PACK, H // 2], F32, 40)
-        raw_carry0 = placed("raw_carry0", [P, PACK, H], F32, 46)
-        raw_carry1 = placed("raw_carry1", [P, PACK, H], F32, 54)
-        wev = placed("wev", [P, N], U32, 62)
-        wvol = placed("wvol", [P, 2 * N], U8, 65)
-        wev_plane = placed("wev_plane", [P, N], U8, 67)
-        wvol_plane = placed("wvol_plane", [P, N], U8, 68)
+        tab = [placed(f"tab{a}", [P, T], U32, 16 * a) for a in range(PASSES)]
+        staging = placed("staging", [P, 43 * KIB], U8, 32)
+        raw_carry = [[placed(f"raw_carry{c}{a}", [P, PACK, CHUNK], F32, 36 + 8 * c + 4 * a if c + a else 112) for a in range(PASSES)] for c in range(CHUNKS)]
+        raw_day = [placed(f"raw_day{a}", [P, PACK, H], F32, 52 + 8 * a) for a in range(PASSES)]
+        wev = placed("wev", [P, N], U32, 68)
+        wvol = placed("wvol", [P, 2 * N], U8, 71)
+        wev_plane = placed("wev_plane", [P, N], U8, 73)
+        wvol_plane = placed("wvol_plane", [P, N], U8, 74)
 
         def load_w1(raw, a, first):
             rows = w1[a * P * PACK : (a + 1) * P * PACK, first : first + raw.shape[2]]
@@ -73,89 +74,33 @@ def tile_list_skimming_triage_kernel(
         def load_tab(a):
             nc.sync.dma_start(out=tab[a][:].bitcast(I32), in_=tab_words[a].rearrange("p t i -> p (t i)").bitcast(I32))
 
-        v_words = [placed(f"v_words{a}", [P, S], U32, 104 - 4 * a) for a in range(PASSES)]
+        v_words = [placed(f"v_words{a}", [P, S], U32, 88 + 4 * a) for a in range(PASSES)]
         v_rows = keep.tile([P, S], U8, name="v_rows", align_bytes=64)
-        v_planes = [keep.tile([P, S], U8, name="v_plane0", align_bytes=64), placed("v_plane1", [P, S], U8, 44)]
+        v_plane = keep.tile([P, PASSES * S], U8, name="v_plane", align_bytes=64)
 
         nc.vector.memset(staging[QUADRANT : 2 * QUADRANT, :T].bitcast(I32), 0)
         nc.vector.memset(staging[2 * QUADRANT :, :T].bitcast(I32), 0)
         nc.sync.dma_start(offs_sb[:], offs)
-        nc.sync.dma_start(out=staging[:QUADRANT, :T].bitcast(I32), in_=tab_scales.rearrange("a q t -> (a q) t").bitcast(I32))
-        load_w1(raw_day0, 0, 0)
+        nc.sync.dma_start(out=staging[:QUADRANT, :T].bitcast(I32), in_=tab_scales.rearrange("a q t -> q a t").bitcast(I32))
+        load_tab(0)
         nc.sync.dma_start(pos1_sb[:], pos1)
         nc.sync.dma_start(pos2_sb[:], pos2)
         nc.sync.dma_start(pos3_sb[:], pos3)
-        load_tab(0)
-        nc.vector.tensor_copy(v_rows[:], staging[:, :T].indirect(offs_sb[:]))
-        rows_per_pass = QUADRANT // PASSES
-
-        def move_scales(a):
-            for i in range(PACK):
-                nc.sync.dma_start(
-                    out=v_planes[a][PACK * a + i :: QUADRANT, :].bitcast(I32),
-                    in_=v_rows[rows_per_pass * a + i : rows_per_pass * (a + 1) : PACK, :].bitcast(I32),
-                )
-
-        move_scales(0)
+        load_w1(raw_carry[0][0], 0, H)
         load_tab(1)
-        move_scales(1)
-        load_w1(raw_day1a, 1, 0)
-
-        big = keep.tile([P, 1], F32, name="big")
-        one = keep.tile([P, 1], F32, name="one")
-        nc.vector.memset(big[:], SATURATED)
-        nc.scalar.activation(one[:], big[:], ACT.Sigmoid)
-
-        grouped = [[placed(f"grouped{c}{a}", [P, PACK, P, PACK], BF16, 72 + 8 * c + 4 * a) for a in range(PASSES)] for c in range(2)]
-        w_words = [
-            [placed("w_words00", [P, H], U32, 0) if (c, a) == (DAY, 0) else keep.tile([P, H], U32, name=f"w_words{c}{a}", align_bytes=64) for a in range(PASSES)]
-            for c in range(2)
-        ]
-        w_plane = [[keep.tile([P, H], U8, name=f"w_plane{c}{a}", align_bytes=64) for a in range(PASSES)] for c in range(2)]
-
-        def group_w1(raw, c, a, first, scalar_share):
-            count = raw.shape[2] // PACK
-            src = raw[:].rearrange("p j (m t) -> p m j t", t=PACK)
-            dst = grouped[c][a][:].rearrange("p t m j -> p m j t")[:, first : first + count]
-            if scalar_share > 0:
-                nc.scalar.copy(dst[:, :scalar_share], src[:, :scalar_share])
-            if scalar_share < count:
-                nc.vector.tensor_copy(dst[:, scalar_share:], src[:, scalar_share:])
-
-        def quantize_w1(c, a, calls):
-            flat = grouped[c][a][:].rearrange("p t m j -> p (t m j)")
-            width = H // calls
-            for i in range(calls):
-                cols = slice(i * width, (i + 1) * width)
-                nc.vector.quantize_mx(
-                    out=w_words[c][a][:, cols].bitcast(FP8X4),
-                    scales=w_plane[c][a][:, cols],
-                    in_=flat[:, PACK * i * width : PACK * (i + 1) * width],
-                )
-
-        def stage1_pass(bank, c, a, t, half):
-            rows = slice(t * P, (t + 1) * P)
-            nc.tensor.matmul_mx(
-                out=bank[:],
-                lhsT=w_words[c][a][:, rows].bitcast(FP8X4),
-                lhsT_scale=w_plane[c][a][:, rows],
-                rhs=v_words[a][:, half * BANK : (half + 1) * BANK].bitcast(FP8X4),
-                rhs_scale=v_planes[a][PACK * a :, half * BANK : (half + 1) * BANK],
-                start=(a == 0),
-                stop=(a == PASSES - 1),
+        nc.vector.tensor_copy(v_rows[:], staging[:, :T].indirect(offs_sb[:]))
+        rows_per_quadrant = PACK * PASSES
+        for q in range(P // QUADRANT):
+            nc.sync.dma_start(
+                out=v_plane[QUADRANT * q : QUADRANT * q + PACK, :].bitcast(I32),
+                in_=v_rows[rows_per_quadrant * q : rows_per_quadrant * (q + 1), :].bitcast(I32),
             )
-
-        h = [[keep.tile([P, S], F32, name=f"h{c}{t}", align_bytes=64) for t in range(PACK)] for c in range(2)]
-        places = [(t, half) for t in range(PACK) for half in range(2)]
-
-        group_w1(raw_day0, DAY, 0, 0, P)
-        load_w1(raw_day1b, 1, H // 2)
-        nc.vector.tensor_copy(v_words[0][:], tab[0][:].indirect(offs_sb[:]))
-        quantize_w1(DAY, 0, 1)
-        load_w1(raw_carry0, 0, H)
-        load_w1(raw_carry1, 1, H)
-
-        nc.vector.tensor_copy(v_words[1][:], tab[1][:].indirect(offs_sb[:]))
+        for c in range(CHUNKS):
+            for a in range(PASSES):
+                if c + a:
+                    load_w1(raw_carry[c][a], a, H + c * CHUNK)
+        for a in range(PASSES):
+            load_w1(raw_day[a], a, 0)
         nc.sync.dma_start(out=wev[:].bitcast(I32), in_=wev_words[0].rearrange("p c i -> p (c i)").bitcast(I32))
         nc.sync.dma_start(out=wvol[:].bitcast(I32), in_=wvol_words[0].bitcast(I32))
         for plane, scales in ((wev_plane, wev_scales), (wvol_plane, wvol_scales)):
@@ -165,84 +110,131 @@ def tile_list_skimming_triage_kernel(
                     in_=scales[0, PACK * q : PACK * (q + 1), :].bitcast(I32),
                 )
 
-        group_w1(raw_day1a, DAY, 1, 0, P // 2)
-        group_w1(raw_day1b, DAY, 1, P // 2, LAST_SCALAR_SHARE)
-        quantize_w1(DAY, 1, PACK)
-        day_banks = {place: psum.tile([P, BANK], F32, name="bank") for place in places}
+        big = keep.tile([P, 1], F32, name="big")
+        one = keep.tile([P, 1], F32, name="one")
+        nc.vector.memset(big[:], SATURATED)
+        minus_two = placed("minus_two", [P, 1], F32, 120)
+        nc.vector.memset(minus_two[:], -2.0)
+        nc.scalar.activation(one[:], big[:], ACT.Sigmoid)
+
         for a in range(PASSES):
-            for t, half in places:
-                stage1_pass(day_banks[t, half], DAY, a, t, half)
+            nc.vector.tensor_copy(v_words[a][:], tab[a][:].indirect(offs_sb[:]))
 
-        def empty(c, t, half, bank, on_vector):
-            dst = h[c][t][:, half * BANK : (half + 1) * BANK]
-            if c == DAY and on_vector:
-                nc.vector.tensor_scalar(dst, bank[:], 0.5, 0.5, ALU.mult, ALU.add)
-            elif c == DAY:
-                nc.scalar.activation(dst, bank[:], ACT.Copy, scale=0.5, bias=0.5)
-            elif on_vector:
-                nc.vector.tensor_copy(dst, bank[:])
-            else:
-                nc.scalar.copy(dst, bank[:])
+        def regrouped(name, raw, scalar_share):
+            count = raw.shape[2] // PACK
+            grouped = keep.tile([P, PACK, count, PACK], BF16, name=name + "_grouped", align_bytes=64)
+            src = raw[:].rearrange("p j (m t) -> p m j t", t=PACK)
+            dst = grouped[:].rearrange("p t m j -> p m j t")
+            if scalar_share > 0:
+                nc.scalar.copy(dst[:, :scalar_share], src[:, :scalar_share])
+            if scalar_share < count:
+                nc.vector.tensor_copy(dst[:, scalar_share:], src[:, scalar_share:])
+            return grouped[:].rearrange("p t m j -> p (t m j)")
 
-        for t, half in VECTOR_DAY_BANKS:
-            empty(DAY, t, half, day_banks[t, half], True)
-        for a, raw in enumerate((raw_carry0, raw_carry1)):
-            group_w1(raw, CARRY, a, 0, 0)
-            quantize_w1(CARRY, a, 1)
+        def quantized(name, values, kib=None):
+            width = values.shape[1] // PACK
+            words = keep.tile([P, width], U32, name=name + "_words", align_bytes=64) if kib is None else placed(name + "_words", [P, width], U32, kib)
+            plane = keep.tile([P, width], U8, name=name + "_plane", align_bytes=64)
+            nc.vector.quantize_mx(out=words[:].bitcast(FP8X4), scales=plane[:], in_=values)
+            return [(words[:, i : i + P], plane[:, i : i + P]) for i in range(0, width, P)]
 
-        sig = [
-            [keep.tile([P, M_PART], F32, name=f"sig0{t}", align_bytes=64) for t in range(PACK)],
-            [placed(f"sig1{t}", [P, M_PART], F32, 84 + t) for t in range(PACK)],
+        def stage1_bank(weights, block, half):
+            bank = psum.tile([P, BANK], F32, name="bank")
+            for a in range(PASSES):
+                words, plane = weights[a][block]
+                nc.tensor.matmul_mx(
+                    out=bank[:],
+                    lhsT=words.bitcast(FP8X4),
+                    lhsT_scale=plane,
+                    rhs=v_words[a][:, half * BANK : (half + 1) * BANK].bitcast(FP8X4),
+                    rhs_scale=v_plane[:, a * S + half * BANK : a * S + (half + 1) * BANK],
+                    start=(a == 0),
+                    stop=(a == PASSES - 1),
+                )
+            return bank
+
+        first = quantized("carry00", regrouped("carry00", raw_carry[0][0], CHUNK // PACK))
+        second = regrouped("carry01", raw_carry[0][1], C01_SCALAR)
+        carry_weights = [
+            [first, quantized("carry01a", second[:, : P * PACK]) + quantized("carry01b", second[:, P * PACK :])],
+            [quantized(f"carry1{a}", regrouped(f"carry1{a}", raw_carry[1][a], (C10_SCALAR, 0)[a])) for a in range(PASSES)],
         ]
-        diff = [
-            [placed(f"diff0{t}", [P, M_PART], F32, 46 if t == 0 else 54 + t) for t in range(PACK)],
-            [keep.tile([P, M_PART], F32, name=f"diff1{t}", align_bytes=64) for t in range(PACK)],
-        ]
+        day_values = [regrouped("day0", raw_day[0], 0)]
+        lead = [quantized("day0a", day_values[0][:, : 2 * P * PACK])]
+        day_values.append(regrouped("day1", raw_day[1], 0))
+        lead.append(quantized("day1a", day_values[1][:, : 2 * P * PACK]))
+        rest = [quantized(f"day{a}b", day_values[a][:, 2 * P * PACK :], 60 + a) for a in range(PASSES)]
+        day_weights = [lead[a] + rest[a] for a in range(PASSES)]
+
+        picked = keep.tile([P, PACK * M], F32, name="picked", align_bytes=64)
+        away = [keep.tile([P, M], F32, name=f"away{u}", align_bytes=64) for u in range(2)]
+
+        def slot(t):
+            return slice(t * M, (t + 1) * M)
+
+        for c in range(CHUNKS):
+            for u in range(2):
+                carry = keep.tile([P, S], F32, name=f"carry{c}{u}", align_bytes=64)
+                for half in range(2):
+                    bank = stage1_bank(carry_weights[c], u, half)
+                    dst = carry[:, half * BANK : (half + 1) * BANK]
+                    if (c, u, half) in VECTOR_CARRY_BANKS:
+                        nc.vector.tensor_copy(dst, bank[:])
+                    else:
+                        nc.scalar.copy(dst, bank[:])
+                dst = picked[:, slot(2 * u)] if c == 0 else away[u][:]
+                nc.scalar.activation(dst, carry[:].indirect(pos3_sb[:]), ACT.Copy, scale=-2.0)
+                if c == 0:
+                    nc.sync.dma_start(out=picked[:HALF, slot(2 * u + 1)], in_=picked[HALF:, slot(2 * u)])
+                else:
+                    nc.sync.dma_start(out=picked[HALF:, slot(2 * u)], in_=away[u][:HALF, :])
+                    nc.sync.dma_start(out=picked[HALF:, slot(2 * u + 1)], in_=away[u][HALF:, :])
 
         def columns(part):
             return slice(part * M_PART // LIST_ROWS, (part + 1) * M_PART // LIST_ROWS)
 
+        day = [keep.tile([P, S], F32, name=f"day{t}", align_bytes=64) for t in range(PACK)]
+        sig = [[placed(f"sig{part}{t}", [P, M_PART], F32, 76 + t) for t in range(PACK)] for part in range(PARTS)]
+        diff = [placed(f"diff{part}", [P, PACK, M_PART], F32, 100 + 4 * part) for part in range(PARTS)]
+
         def squash(part, t):
-            nc.scalar.activation(sig[part][t][:], h[DAY][t][:].indirect(pos1_sb[:, columns(part)]), ACT.Sigmoid, scale=4.0, bias=-2.0)
+            nc.scalar.activation(sig[part][t][:], day[t][:].indirect(pos1_sb[:, columns(part)]), ACT.Sigmoid, scale=4.0, bias=minus_two[:])
 
         def differ(part, t):
-            nc.vector.tensor_tensor(diff[part][t][:], h[DAY][t][:].indirect(pos2_sb[:, columns(part)]), sig[part][t][:], ALU.subtract)
+            nc.vector.tensor_tensor(diff[part][:, t, :], day[t][:].indirect(pos2_sb[:, columns(part)]), sig[part][t][:], ALU.subtract)
 
         for t in range(PACK):
             for half in range(2):
-                if (t, half) not in VECTOR_DAY_BANKS:
-                    empty(DAY, t, half, day_banks[t, half], False)
+                bank = stage1_bank(day_weights, t, half)
+                dst = day[t][:, half * BANK : (half + 1) * BANK]
+                if (t, half) in VECTOR_DAY_BANKS:
+                    nc.vector.tensor_scalar(dst, bank[:], 0.5, 0.5, ALU.mult, ALU.add)
+                else:
+                    nc.scalar.activation(dst, bank[:], ACT.Copy, scale=0.5, bias=0.5)
+        for t in range(PACK):
             squash(0, t)
             differ(0, t)
-
-        for t, half in places:
-            bank = psum.tile([P, BANK], F32, name="bank")
-            for a in range(PASSES):
-                stage1_pass(bank, CARRY, a, t, half)
-            empty(CARRY, t, half, bank, (t, half) in VECTOR_CARRY_BANKS)
-
         for t in range(PACK):
             squash(1, t)
-        one_again = placed("one_again", [P, 1], F32, 100)
+
+        one_again = placed("one_again", [P, 1], F32, 120)
         nc.scalar.activation(one_again[:], one[:], ACT.Abs_reciprocal_sqrt)
 
         groups = range(N // P // GROUP)
         for part in range(PARTS):
             last_part = part == PARTS - 1
             cases = slice(part * M_PART, (part + 1) * M_PART)
-            neg_z = placed(f"neg_z{part}", [P, PACK, M_PART], F32, 116 + 4 * part)
-            for t in range(PACK):
-                nc.vector.tensor_tensor(neg_z[:, t, :], h[CARRY][t][:].indirect(pos3_sb[:, columns(part)]), diff[part][t][:], ALU.mult)
-            z_bf = placed(f"z_bf{part}", [P, M_PART, PACK], BF16, 120 + 4 * part)
+            z_bf = placed(f"z_bf{part}", [P, M_PART, PACK], BF16, 104 + 4 * part)
             z_words = keep.tile([P, M_PART], U32, name=f"z_words{part}", align_bytes=64)
             z_plane = keep.tile([P, M_PART], U8, name=f"z_plane{part}", align_bytes=64)
             z_pieces = 2 if last_part else 1
             z_spans = [slice(i * M_PART // z_pieces, (i + 1) * M_PART // z_pieces) for i in range(z_pieces)]
             for cols in z_spans:
-                nc.vector.tensor_scalar(
+                nc.vector.tensor_tensor(
                     z_bf[:, cols, :].rearrange("p (c i) t -> p c t i", i=PACK),
-                    neg_z[:, :, cols].rearrange("p t (c i) -> p c t i", i=PACK),
-                    -2.0, None, ALU.mult,
+                    diff[part][:, :, cols].rearrange("p t (c i) -> p c t i", i=PACK),
+                    picked[:].rearrange("p (t m) -> p t m", t=PACK)[:, :, cases][:, :, cols].rearrange("p t (c i) -> p c t i", i=PACK),
+                    ALU.mult,
                 )
             for cols in z_spans:
                 nc.vector.quantize_mx(

@@ -48,12 +48,15 @@ def tile_list_skimming_triage_kernel(
         keep = ctx.enter_context(tc.tile_pool(name="keep", bufs=1))
         reuse = ctx.enter_context(tc.tile_pool(name="reuse", bufs=1))
         ring = ctx.enter_context(tc.tile_pool(name="ring", bufs=4))
+        far = ctx.enter_context(tc.tile_pool(name="far", bufs=1))
         psum = ctx.enter_context(tc.psum_pool(name="psum", bufs=8))
 
         offs_sb = lists.tile([P, S // LIST_ROWS], U16, name="offs_sb")
         pos1_sb = lists.tile([P, M // LIST_ROWS], U16, name="pos1_sb")
         pos2_sb = lists.tile([P, M // LIST_ROWS], U16, name="pos2_sb")
         pos3_sb = lists.tile([P, M // LIST_ROWS], U16, name="pos3_sb")
+
+        first_day = keep.tile([P, S], F32, name="day0", align_bytes=64)
 
         def placed(name, shape, dtype, kib):
             return reuse.tile(shape, dtype, name=name, align_bytes=64, offset=int(kib * KIB))
@@ -174,7 +177,7 @@ def tile_list_skimming_triage_kernel(
 
         for c in range(CHUNKS):
             for u in range(2):
-                carry = keep.tile([P, S], F32, name=f"carry{c}{u}", align_bytes=64)
+                carry = far.tile([P, S], F32, name=f"carry{c}{u}", align_bytes=64)
                 for half in range(2):
                     bank = stage1_bank(carry_weights[c], u, half)
                     dst = carry[:, half * BANK : (half + 1) * BANK]
@@ -193,7 +196,7 @@ def tile_list_skimming_triage_kernel(
         def columns(part):
             return slice(part * M_PART // LIST_ROWS, (part + 1) * M_PART // LIST_ROWS)
 
-        day = [keep.tile([P, S], F32, name=f"day{t}", align_bytes=64) for t in range(PACK)]
+        day = [first_day, placed("day1", [P, S], F32, 20), placed("day2", [P, S], F32, 84), far.tile([P, S], F32, name="day3", align_bytes=64)]
         sig = [[placed(f"sig{part}{t}", [P, M_PART], F32, 76 + t) for t in range(PACK)] for part in range(PARTS)]
         diff = [placed(f"diff{part}", [P, PACK, M_PART], F32, 100 + 4 * part) for part in range(PARTS)]
 

@@ -175,23 +175,34 @@ def tile_list_skimming_triage_kernel(
         def slot(t):
             return slice(t * M, (t + 1) * M)
 
-        for c in range(CHUNKS):
-            for u in range(2):
-                carry = far.tile([P, S], F32, name=f"carry{c}{u}", align_bytes=64)
-                for half in range(2):
-                    bank = stage1_bank(carry_weights[c], u, half)
-                    dst = carry[:, half * BANK : (half + 1) * BANK]
-                    if (c, u, half) in VECTOR_CARRY_BANKS:
-                        nc.vector.tensor_copy(dst, bank[:])
-                    else:
-                        nc.scalar.copy(dst, bank[:])
-                dst = picked[:, slot(2 * u)] if c == 0 else away[u][:]
-                nc.scalar.activation(dst, carry[:].indirect(pos3_sb[:]), ACT.Copy, scale=-2.0)
-                if c == 0:
-                    nc.sync.dma_start(out=picked[:HALF, slot(2 * u + 1)], in_=picked[HALF:, slot(2 * u)])
+        carry = [[far.tile([P, S], F32, name=f"carry{c}{u}", align_bytes=64) for u in range(2)] for c in range(CHUNKS)]
+
+        def empty_carry(c, u):
+            for half in range(2):
+                bank = stage1_bank(carry_weights[c], u, half)
+                dst = carry[c][u][:, half * BANK : (half + 1) * BANK]
+                if (c, u, half) in VECTOR_CARRY_BANKS:
+                    nc.vector.tensor_copy(dst, bank[:])
                 else:
-                    nc.sync.dma_start(out=picked[HALF:, slot(2 * u)], in_=away[u][:HALF, :])
-                    nc.sync.dma_start(out=picked[HALF:, slot(2 * u + 1)], in_=away[u][HALF:, :])
+                    nc.scalar.copy(dst, bank[:])
+
+        def pick(c, u):
+            dst = picked[:, slot(2 * u)] if c == 0 else away[u][:]
+            nc.scalar.activation(dst, carry[c][u][:].indirect(pos3_sb[:]), ACT.Copy, scale=-2.0)
+            if c == 0:
+                nc.sync.dma_start(out=picked[:HALF, slot(2 * u + 1)], in_=picked[HALF:, slot(2 * u)])
+            else:
+                nc.sync.dma_start(out=picked[HALF:, slot(2 * u)], in_=away[u][:HALF, :])
+                nc.sync.dma_start(out=picked[HALF:, slot(2 * u + 1)], in_=away[u][HALF:, :])
+
+        empty_carry(0, 0)
+        empty_carry(0, 1)
+        pick(0, 0)
+        empty_carry(1, 0)
+        pick(0, 1)
+        empty_carry(1, 1)
+        pick(1, 0)
+        pick(1, 1)
 
         def columns(part):
             return slice(part * M_PART // LIST_ROWS, (part + 1) * M_PART // LIST_ROWS)
@@ -204,7 +215,12 @@ def tile_list_skimming_triage_kernel(
             nc.scalar.activation(sig[part][t][:], day[t][:].indirect(pos1_sb[:, columns(part)]), ACT.Sigmoid, scale=4.0, bias=minus_two[:])
 
         def differ(part, t):
-            nc.vector.tensor_tensor(diff[part][:, t, :], day[t][:].indirect(pos2_sb[:, columns(part)]), sig[part][t][:], ALU.subtract)
+            pieces = 2 if t == PACK - 1 else 1
+            width = M_PART // pieces
+            for first in range(0, M_PART, width):
+                entries = slice((part * M_PART + first) // LIST_ROWS, (part * M_PART + first + width) // LIST_ROWS)
+                cols = slice(first, first + width)
+                nc.vector.tensor_tensor(diff[part][:, t, cols], day[t][:].indirect(pos2_sb[:, entries]), sig[part][t][:, cols], ALU.subtract)
 
         for t in range(PACK):
             for half in range(2):
@@ -230,7 +246,7 @@ def tile_list_skimming_triage_kernel(
             z_bf = placed(f"z_bf{part}", [P, M_PART, PACK], BF16, 104 + 4 * part)
             z_words = keep.tile([P, M_PART], U32, name=f"z_words{part}", align_bytes=64)
             z_plane = keep.tile([P, M_PART], U8, name=f"z_plane{part}", align_bytes=64)
-            z_pieces = 2 if last_part else 1
+            z_pieces = 2
             z_spans = [slice(i * M_PART // z_pieces, (i + 1) * M_PART // z_pieces) for i in range(z_pieces)]
             for cols in z_spans:
                 nc.vector.tensor_tensor(
@@ -264,32 +280,58 @@ def tile_list_skimming_triage_kernel(
                         lhsT=wev[:, n0 : n0 + P].bitcast(FP8X4), lhsT_scale=wev_plane[:, n0 : n0 + P],
                         rhs=z_words[:].bitcast(FP8X4), rhs_scale=z_plane[:], start=True, stop=True,
                     )
-            for g in groups:
-                size = ring.tile([P, BANK], F32, name="size")
-                root = ring.tile([P, BANK], F32, name="root")
-                between = ring.tile([P, BANK], F32, name="between")
-                res = ring.tile([P, BANK], F32, name="res")
-                nc.scalar.activation(size[:], vols[g][:], ACT.Abs)
-                last_group = g == groups[-1]
-                scalar_squares = last_group == last_part
-                pieces = GROUP if last_part or not scalar_squares else 1
-                width = BANK // pieces
-                spans = [slice(i * width, (i + 1) * width) for i in range(pieces)]
-                for cols in spans if last_part and last_group else [slice(0, BANK)]:
-                    nc.scalar.activation(root[:, cols], size[:, cols], ACT.Abs_reciprocal_sqrt, bias=one_again[:])
+            size = [ring.tile([P, BANK], F32, name="size") for g in groups]
+            root = [ring.tile([P, BANK], F32, name="root") for g in groups]
+            between = [ring.tile([P, BANK], F32, name="between") for g in groups]
+            res = [ring.tile([P, BANK], F32, name="res") for g in groups]
+            whole = [slice(0, BANK)]
+            tiles = [slice(i * M_PART, (i + 1) * M_PART) for i in range(GROUP)]
+
+            def absolute(g):
+                nc.scalar.activation(size[g][:], vols[g][:], ACT.Abs)
+
+            def inverse_root(g, spans):
                 for cols in spans:
-                    if scalar_squares:
-                        nc.scalar.activation(between[:, cols], root[:, cols], ACT.Square)
-                    else:
-                        nc.vector.tensor_tensor(between[:, cols], evs[g][:, cols], root[:, cols], ALU.mult)
-                for i, cols in enumerate(spans):
-                    if scalar_squares:
-                        nc.vector.tensor_tensor(res[:, cols], evs[g][:, cols], between[:, cols], ALU.mult)
-                    else:
-                        nc.vector.tensor_tensor(res[:, cols], between[:, cols], root[:, cols], ALU.mult)
-                    tiles = GROUP // pieces
-                    first = (g * GROUP + i * tiles) * P
+                    nc.scalar.activation(root[g][:, cols], size[g][:, cols], ACT.Abs_reciprocal_sqrt, bias=one_again[:])
+
+            def square(g, spans):
+                for cols in spans:
+                    nc.scalar.activation(between[g][:, cols], root[g][:, cols], ACT.Square)
+
+            def once(g, spans):
+                for cols in spans:
+                    nc.vector.tensor_tensor(between[g][:, cols], evs[g][:, cols], root[g][:, cols], ALU.mult)
+
+            def finish(g, spans, squared):
+                for cols in spans:
+                    other = evs[g] if squared else root[g]
+                    nc.vector.tensor_tensor(res[g][:, cols], other[:, cols], between[g][:, cols], ALU.mult)
+                    count = (cols.stop - cols.start) // M_PART
+                    first = (g * GROUP + cols.start // M_PART) * P
                     nc.sync.dma_start(
-                        out=out[first : first + tiles * P, cases].rearrange("(i p) m -> p i m", p=P),
-                        in_=res[:, cols].rearrange("p (i m) -> p i m", i=tiles),
+                        out=out[first : first + count * P, cases].rearrange("(i p) m -> p i m", p=P),
+                        in_=res[g][:, cols].rearrange("p (i m) -> p i m", i=count),
                     )
+
+            absolute(0)
+            absolute(1)
+            inverse_root(0, whole)
+            absolute(2)
+            inverse_root(1, whole)
+            if last_part:
+                inverse_root(2, tiles)
+                square(2, tiles)
+                for g in (0, 1):
+                    once(g, tiles)
+                    finish(g, tiles, False)
+                finish(2, tiles, True)
+            else:
+                square(0, whole)
+                inverse_root(2, whole)
+                square(1, tiles[:1])
+                once(2, whole)
+                finish(0, whole, True)
+                finish(2, whole, False)
+                once(1, tiles[1:])
+                finish(1, tiles[:1], True)
+                finish(1, tiles[1:], False)

@@ -21,6 +21,7 @@ PACK = 4
 PASSES = K // (P * PACK)
 BANK = 512
 QUADRANT = 32
+QUADRANT_ORDER = (0, 2, 1, 3)
 LIST_ROWS = 16
 KIB = 1024
 DAY, CARRY = 0, 1
@@ -93,8 +94,8 @@ def tile_list_skimming_triage_kernel(
         load_tab(1)
         nc.vector.tensor_copy(v_rows[:], staging[:, :T].indirect(offs_sb[:]))
         rows_per_quadrant = PACK * PASSES
-        for q in range(P // QUADRANT):
-            nc.sync.dma_start(
+        for q in QUADRANT_ORDER:
+            nc.gpsimd.dma_start(
                 out=v_plane[QUADRANT * q : QUADRANT * q + PACK, :].bitcast(I32),
                 in_=v_rows[rows_per_quadrant * q : rows_per_quadrant * (q + 1), :].bitcast(I32),
             )
@@ -107,7 +108,7 @@ def tile_list_skimming_triage_kernel(
         nc.sync.dma_start(out=wev[:].bitcast(I32), in_=wev_words[0].rearrange("p c i -> p (c i)").bitcast(I32))
         nc.sync.dma_start(out=wvol[:].bitcast(I32), in_=wvol_words[0].bitcast(I32))
         for plane, scales in ((wev_plane, wev_scales), (wvol_plane, wvol_scales)):
-            for q in range(P // QUADRANT):
+            for q in QUADRANT_ORDER:
                 nc.sync.dma_start(
                     out=plane[QUADRANT * q : QUADRANT * q + PACK, :].bitcast(I32),
                     in_=scales[0, PACK * q : PACK * (q + 1), :].bitcast(I32),

@@ -63,7 +63,7 @@ def tile_list_skimming_triage_kernel(
             return reuse.tile(shape, dtype, name=name, align_bytes=64, offset=int(kib * KIB))
 
         tab = [placed(f"tab{a}", [P, T], U32, 16 * a) for a in range(PASSES)]
-        staging = placed("staging", [P, 43 * KIB], U8, 32)
+        staging = placed("staging", [P, T], U8, 32)
         raw_carry = [[placed(f"raw_carry{c}{a}", [P, PACK, CHUNK], F32, 36 + 8 * c + 4 * a if c + a else 112) for a in range(PASSES)] for c in range(CHUNKS)]
         raw_day = [placed(f"raw_day{a}", [P, PACK, H], F32, 52 + 8 * a) for a in range(PASSES)]
         wev = placed("wev", [P, N], U32, 68)
@@ -82,17 +82,14 @@ def tile_list_skimming_triage_kernel(
         v_rows = keep.tile([P, S], U8, name="v_rows", align_bytes=64)
         v_plane = keep.tile([P, PASSES * S], U8, name="v_plane", align_bytes=64)
 
-        nc.vector.memset(staging[QUADRANT : 2 * QUADRANT, :T].bitcast(I32), 0)
-        nc.vector.memset(staging[2 * QUADRANT :, :T].bitcast(I32), 0)
+        nc.vector.memset(staging[QUADRANT : 2 * QUADRANT, :].bitcast(I32), 0)
+        nc.vector.memset(staging[2 * QUADRANT :, :].bitcast(I32), 0)
         nc.sync.dma_start(offs_sb[:], offs)
-        nc.sync.dma_start(out=staging[:QUADRANT, :T].bitcast(I32), in_=tab_scales.rearrange("a q t -> q a t").bitcast(I32))
+        nc.sync.dma_start(out=staging[:QUADRANT, :].bitcast(I32), in_=tab_scales.rearrange("a q t -> q a t").bitcast(I32))
         load_tab(0)
-        nc.sync.dma_start(pos1_sb[:], pos1)
-        nc.sync.dma_start(pos2_sb[:], pos2)
-        nc.sync.dma_start(pos3_sb[:], pos3)
         load_w1(raw_carry[0][0], 0, H)
         load_tab(1)
-        nc.vector.tensor_copy(v_rows[:], staging[:, :T].indirect(offs_sb[:]))
+        nc.vector.tensor_copy(v_rows[:], staging[:].indirect(offs_sb[:]))
         rows_per_quadrant = PACK * PASSES
         for q in QUADRANT_ORDER:
             nc.gpsimd.dma_start(
@@ -103,8 +100,11 @@ def tile_list_skimming_triage_kernel(
             for a in range(PASSES):
                 if c + a:
                     load_w1(raw_carry[c][a], a, H + c * CHUNK)
+        nc.sync.dma_start(pos3_sb[:], pos3)
         for a in range(PASSES):
             load_w1(raw_day[a], a, 0)
+        nc.sync.dma_start(pos1_sb[:], pos1)
+        nc.sync.dma_start(pos2_sb[:], pos2)
         nc.sync.dma_start(out=wev[:].bitcast(I32), in_=wev_words[0].rearrange("p c i -> p (c i)").bitcast(I32))
         nc.sync.dma_start(out=wvol[:].bitcast(I32), in_=wvol_words[0].bitcast(I32))
         for plane, scales in ((wev_plane, wev_scales), (wvol_plane, wvol_scales)):

from contextlib import ExitStack

import concourse.mybir as mybir

K, T, S, H, M, N = 1024, 4096, 1024, 512, 512, 768
FLOPS = 2 * K * 2 * H * S + 2 * 2 * H * N * M

F32 = mybir.dt.float32
BF16 = mybir.dt.bfloat16
I32 = mybir.dt.int32
U32 = mybir.dt.uint32
U16 = mybir.dt.uint16
U8 = mybir.dt.uint8
FP8X4 = mybir.dt.float8_e4m3fn_x4
FP4X4 = mybir.dt.float4_e2m1fn_x4
ACT = mybir.ActivationFunctionType
ALU = mybir.AluOpType

P = 128
PACK = 4
PASSES = K // (P * PACK)
BANK = 512
QUADRANT = 32
QUADRANT_ORDER = (0, 2, 1, 3)
LIST_ROWS = 16
KIB = 1024
DAY, CARRY = 0, 1

M_PART = 256
PARTS = M // M_PART
GROUP = BANK // M_PART

HALF = P // 2
CHUNKS = 2
CHUNK = H // CHUNKS
SATURATED = 64.0
C01_SCALAR = 64
C10_SCALAR = 40
VECTOR_CARRY_BANKS = ((0, 1, 0), (0, 1, 1))
VECTOR_DAY_BANKS = ((0, 0), (0, 1), (1, 0), (1, 1), (2, 0), (2, 1), (3, 1))


def tile_list_skimming_triage_kernel(
    tc, tab_words, tab_scales, offs, pos1, pos2, pos3, w1, wev_words, wev_scales, wvol_words, wvol_scales, out
):
    nc = tc.nc
    with ExitStack() as ctx:
        lists = ctx.enter_context(tc.tile_pool(name="lists", bufs=1))
        keep = ctx.enter_context(tc.tile_pool(name="keep", bufs=1))
        reuse = ctx.enter_context(tc.tile_pool(name="reuse", bufs=1))
        ring = ctx.enter_context(tc.tile_pool(name="ring", bufs=4))
        far = ctx.enter_context(tc.tile_pool(name="far", bufs=1))
        psum = ctx.enter_context(tc.psum_pool(name="psum", bufs=8))

        offs_sb = lists.tile([P, S // LIST_ROWS], U16, name="offs_sb")
        pos1_sb = lists.tile([P, M // LIST_ROWS], U16, name="pos1_sb")
        pos2_sb = lists.tile([P, M // LIST_ROWS], U16, name="pos2_sb")
        pos3_sb = lists.tile([P, M // LIST_ROWS], U16, name="pos3_sb")

        first_day = keep.tile([P, S], F32, name="day0", align_bytes=64)

        def placed(name, shape, dtype, kib):
            return reuse.tile(shape, dtype, name=name, align_bytes=64, offset=int(kib * KIB))

        tab = [placed(f"tab{a}", [P, T], U32, 16 * a) for a in range(PASSES)]
        staging = placed("staging", [P, T], U8, 32)
        raw_carry = [[placed(f"raw_carry{c}{a}", [P, PACK, CHUNK], F32, 36 + 8 * c + 4 * a if c + a else 112) for a in range(PASSES)] for c in range(CHUNKS)]
        raw_day = [placed(f"raw_day{a}", [P, PACK, H], F32, 52 + 8 * a) for a in range(PASSES)]
        wev = placed("wev", [P, N], U32, 68)
        wvol = placed("wvol", [P, 2 * N], U8, 71)
        wev_plane = placed("wev_plane", [P, N], U8, 73)
        wvol_plane = placed("wvol_plane", [P, N], U8, 74)

        def load_w1(raw, a, first):
            rows = w1[a * P * PACK : (a + 1) * P * PACK, first : first + raw.shape[2]]
            nc.sync.dma_start(out=raw[:], in_=rows.rearrange("(p j) r -> p j r", j=PACK))

        def load_tab(a):
            nc.sync.dma_start(out=tab[a][:].bitcast(I32), in_=tab_words[a].rearrange("p t i -> p (t i)").bitcast(I32))

        v_words = [placed(f"v_words{a}", [P, S], U32, 88 + 4 * a) for a in range(PASSES)]
        v_rows = keep.tile([P, S], U8, name="v_rows", align_bytes=64)
        v_plane = keep.tile([P, PASSES * S], U8, name="v_plane", align_bytes=64)

        nc.vector.memset(staging[QUADRANT : 2 * QUADRANT, :].bitcast(I32), 0)
        nc.vector.memset(staging[2 * QUADRANT :, :].bitcast(I32), 0)
        nc.sync.dma_start(offs_sb[:], offs)
        nc.sync.dma_start(out=staging[:QUADRANT, :].bitcast(I32), in_=tab_scales.rearrange("a q t -> q a t").bitcast(I32))
        load_tab(0)
        load_w1(raw_carry[0][0], 0, H)
        load_tab(1)
        nc.vector.tensor_copy(v_rows[:], staging[:].indirect(offs_sb[:]))
        rows_per_quadrant = PACK * PASSES
        for q in QUADRANT_ORDER:
            nc.gpsimd.dma_start(
                out=v_plane[QUADRANT * q : QUADRANT * q + PACK, :].bitcast(I32),
                in_=v_rows[rows_per_quadrant * q : rows_per_quadrant * (q + 1), :].bitcast(I32),
            )
        for c in range(CHUNKS):
            for a in range(PASSES):
                if c + a:
                    load_w1(raw_carry[c][a], a, H + c * CHUNK)
        nc.sync.dma_start(pos3_sb[:], pos3)
        for a in range(PASSES):
            load_w1(raw_day[a], a, 0)
        nc.sync.dma_start(pos1_sb[:], pos1)
        nc.sync.dma_start(pos2_sb[:], pos2)
        nc.sync.dma_start(out=wev[:].bitcast(I32), in_=wev_words[0].rearrange("p c i -> p (c i)").bitcast(I32))
        nc.sync.dma_start(out=wvol[:].bitcast(I32), in_=wvol_words[0].bitcast(I32))
        for plane, scales in ((wev_plane, wev_scales), (wvol_plane, wvol_scales)):
            for q in QUADRANT_ORDER:
                nc.sync.dma_start(
                    out=plane[QUADRANT * q : QUADRANT * q + PACK, :].bitcast(I32),
                    in_=scales[0, PACK * q : PACK * (q + 1), :].bitcast(I32),
                )

        big = keep.tile([P, 1], F32, name="big")
        one = keep.tile([P, 1], F32, name="one")
        nc.vector.memset(big[:], SATURATED)
        minus_two = placed("minus_two", [P, 1], F32, 120)
        nc.vector.memset(minus_two[:], -2.0)
        nc.scalar.activation(one[:], big[:], ACT.Sigmoid)

        for a in range(PASSES):
            nc.vector.tensor_copy(v_words[a][:], tab[a][:].indirect(offs_sb[:]))

        def regrouped(name, raw, scalar_share):
            count = raw.shape[2] // PACK
            grouped = keep.tile([P, PACK, count, PACK], BF16, name=name + "_grouped", align_bytes=64)
            src = raw[:].rearrange("p j (m t) -> p m j t", t=PACK)
            dst = grouped[:].rearrange("p t m j -> p m j t")
            if scalar_share > 0:
                nc.scalar.copy(dst[:, :scalar_share], src[:, :scalar_share])
            if scalar_share < count:
                nc.vector.tensor_copy(dst[:, scalar_share:], src[:, scalar_share:])
            return grouped[:].rearrange("p t m j -> p (t m j)")

        def quantized(name, values, kib=None):
            width = values.shape[1] // PACK
            words = keep.tile([P, width], U32, name=name + "_words", align_bytes=64) if kib is None else placed(name + "_words", [P, width], U32, kib)
            plane = keep.tile([P, width], U8, name=name + "_plane", align_bytes=64)
            nc.vector.quantize_mx(out=words[:].bitcast(FP8X4), scales=plane[:], in_=values)
            return [(words[:, i : i + P], plane[:, i : i + P]) for i in range(0, width, P)]

        def stage1_bank(weights, block, half):
            bank = psum.tile([P, BANK], F32, name="bank")
            for a in range(PASSES):
                words, plane = weights[a][block]
                nc.tensor.matmul_mx(
                    out=bank[:],
                    lhsT=words.bitcast(FP8X4),
                    lhsT_scale=plane,
                    rhs=v_words[a][:, half * BANK : (half + 1) * BANK].bitcast(FP8X4),
                    rhs_scale=v_plane[:, a * S + half * BANK : a * S + (half + 1) * BANK],
                    start=(a == 0),
                    stop=(a == PASSES - 1),
                )
            return bank

        first = quantized("carry00", regrouped("carry00", raw_carry[0][0], CHUNK // PACK))
        second = regrouped("carry01", raw_carry[0][1], C01_SCALAR)
        carry_weights = [
            [first, quantized("carry01a", second[:, : P * PACK]) + quantized("carry01b", second[:, P * PACK :])],
            [quantized(f"carry1{a}", regrouped(f"carry1{a}", raw_carry[1][a], (C10_SCALAR, 0)[a])) for a in range(PASSES)],
        ]
        day_values = [regrouped("day0", raw_day[0], 0)]
        lead = [quantized("day0a", day_values[0][:, : 2 * P * PACK])]
        day_values.append(regrouped("day1", raw_day[1], 0))
        lead.append(quantized("day1a", day_values[1][:, : 2 * P * PACK]))
        rest = [quantized(f"day{a}b", day_values[a][:, 2 * P * PACK :], 60 + a) for a in range(PASSES)]
        day_weights = [lead[a] + rest[a] for a in range(PASSES)]

        picked = keep.tile([P, PACK * M], F32, name="picked", align_bytes=64)
        away = [keep.tile([P, M], F32, name=f"away{u}", align_bytes=64) for u in range(2)]

        def slot(t):
            return slice(t * M, (t + 1) * M)

        carry = [[far.tile([P, S], F32, name=f"carry{c}{u}", align_bytes=64) for u in range(2)] for c in range(CHUNKS)]

        def empty_carry(c, u):
            for half in range(2):
                bank = stage1_bank(carry_weights[c], u, half)
                dst = carry[c][u][:, half * BANK : (half + 1) * BANK]
                if (c, u, half) in VECTOR_CARRY_BANKS:
                    nc.vector.tensor_copy(dst, bank[:])
                else:
                    nc.scalar.copy(dst, bank[:])

        def pick(c, u):
            dst = picked[:, slot(2 * u)] if c == 0 else away[u][:]
            nc.scalar.activation(dst, carry[c][u][:].indirect(pos3_sb[:]), ACT.Copy, scale=-2.0)
            if c == 0:
                nc.sync.dma_start(out=picked[:HALF, slot(2 * u + 1)], in_=picked[HALF:, slot(2 * u)])
            else:
                nc.sync.dma_start(out=picked[HALF:, slot(2 * u)], in_=away[u][:HALF, :])
                nc.sync.dma_start(out=picked[HALF:, slot(2 * u + 1)], in_=away[u][HALF:, :])

        empty_carry(0, 0)
        empty_carry(0, 1)
        pick(0, 0)
        empty_carry(1, 0)
        pick(0, 1)
        empty_carry(1, 1)
        pick(1, 0)
        pick(1, 1)

        def columns(part):
            return slice(part * M_PART // LIST_ROWS, (part + 1) * M_PART // LIST_ROWS)

        day = [first_day, placed("day1", [P, S], F32, 20), placed("day2", [P, S], F32, 84), far.tile([P, S], F32, name="day3", align_bytes=64)]
        sig = [[placed(f"sig{part}{t}", [P, M_PART], F32, 76 + t) for t in range(PACK)] for part in range(PARTS)]
        diff = [placed(f"diff{part}", [P, PACK, M_PART], F32, 100 + 4 * part) for part in range(PARTS)]

        def squash(part, t):
            nc.scalar.activation(sig[part][t][:], day[t][:].indirect(pos1_sb[:, columns(part)]), ACT.Sigmoid, scale=4.0, bias=minus_two[:])

        def differ(part, t):
            pieces = 2 if t == PACK - 1 else 1
            width = M_PART // pieces
            for first in range(0, M_PART, width):
                entries = slice((part * M_PART + first) // LIST_ROWS, (part * M_PART + first + width) // LIST_ROWS)
                cols = slice(first, first + width)
                nc.vector.tensor_tensor(diff[part][:, t, cols], day[t][:].indirect(pos2_sb[:, entries]), sig[part][t][:, cols], ALU.subtract)

        for t in range(PACK):
            for half in range(2):
                bank = stage1_bank(day_weights, t, half)
                dst = day[t][:, half * BANK : (half + 1) * BANK]
                if (t, half) in VECTOR_DAY_BANKS:
                    nc.vector.tensor_scalar(dst, bank[:], 0.5, 0.5, ALU.mult, ALU.add)
                else:
                    nc.scalar.activation(dst, bank[:], ACT.Copy, scale=0.5, bias=0.5)
        for t in range(PACK):
            squash(0, t)
            differ(0, t)
        for t in range(PACK):
            squash(1, t)

        one_again = placed("one_again", [P, 1], F32, 120)
        nc.scalar.activation(one_again[:], one[:], ACT.Abs_reciprocal_sqrt)

        groups = range(N // P // GROUP)
        for part in range(PARTS):
            last_part = part == PARTS - 1
            cases = slice(part * M_PART, (part + 1) * M_PART)
            z_bf = placed(f"z_bf{part}", [P, M_PART, PACK], BF16, 104 + 4 * part)
            z_words = keep.tile([P, M_PART], U32, name=f"z_words{part}", align_bytes=64)
            z_plane = keep.tile([P, M_PART], U8, name=f"z_plane{part}", align_bytes=64)
            z_pieces = 2
            z_spans = [slice(i * M_PART // z_pieces, (i + 1) * M_PART // z_pieces) for i in range(z_pieces)]
            for cols in z_spans:
                nc.vector.tensor_tensor(
                    z_bf[:, cols, :].rearrange("p (c i) t -> p c t i", i=PACK),
                    diff[part][:, :, cols].rearrange("p t (c i) -> p c t i", i=PACK),
                    picked[:].rearrange("p (t m) -> p t m", t=PACK)[:, :, cases][:, :, cols].rearrange("p t (c i) -> p c t i", i=PACK),
                    ALU.mult,
                )
            for cols in z_spans:
                nc.vector.quantize_mx(
                    out=z_words[:, cols].bitcast(FP8X4), scales=z_plane[:, cols], in_=z_bf[:, cols, :].rearrange("p m t -> p (m t)")
                )
            if not last_part:
                for t in range(PACK):
                    differ(part + 1, t)
            vols = [psum.tile([P, BANK], F32, name="bank") for g in groups]
            evs = [psum.tile([P, BANK], F32, name="bank") for g in groups]
            for g in groups:
                for i in range(GROUP):
                    n0 = (g * GROUP + i) * P
                    nc.tensor.matmul_mx(
                        out=vols[g][:, i * M_PART : (i + 1) * M_PART],
                        lhsT=wvol[:, 2 * n0 : 2 * (n0 + P)].bitcast(FP4X4), lhsT_scale=wvol_plane[:, n0 : n0 + P],
                        rhs=z_words[:].bitcast(FP8X4), rhs_scale=z_plane[:], start=True, stop=True,
                    )
            for g in groups:
                for i in range(GROUP):
                    n0 = (g * GROUP + i) * P
                    nc.tensor.matmul_mx(
                        out=evs[g][:, i * M_PART : (i + 1) * M_PART],
                        lhsT=wev[:, n0 : n0 + P].bitcast(FP8X4), lhsT_scale=wev_plane[:, n0 : n0 + P],
                        rhs=z_words[:].bitcast(FP8X4), rhs_scale=z_plane[:], start=True, stop=True,
                    )
            size = [ring.tile([P, BANK], F32, name="size") for g in groups]
            root = [ring.tile([P, BANK], F32, name="root") for g in groups]
            between = [ring.tile([P, BANK], F32, name="between") for g in groups]
            res = [ring.tile([P, BANK], F32, name="res") for g in groups]
            whole = [slice(0, BANK)]
            tiles = [slice(i * M_PART, (i + 1) * M_PART) for i in range(GROUP)]

            def absolute(g):
                nc.scalar.activation(size[g][:], vols[g][:], ACT.Abs)

            def inverse_root(g, spans):
                for cols in spans:
                    nc.scalar.activation(root[g][:, cols], size[g][:, cols], ACT.Abs_reciprocal_sqrt, bias=one_again[:])

            def square(g, spans):
                for cols in spans:
                    nc.scalar.activation(between[g][:, cols], root[g][:, cols], ACT.Square)

            def once(g, spans):
                for cols in spans:
                    nc.vector.tensor_tensor(between[g][:, cols], evs[g][:, cols], root[g][:, cols], ALU.mult)

            def finish(g, spans, squared):
                for cols in spans:
                    other = evs[g] if squared else root[g]
                    nc.vector.tensor_tensor(res[g][:, cols], other[:, cols], between[g][:, cols], ALU.mult)
                    count = (cols.stop - cols.start) // M_PART
                    first = (g * GROUP + cols.start // M_PART) * P
                    nc.sync.dma_start(
                        out=out[first : first + count * P, cases].rearrange("(i p) m -> p i m", p=P),
                        in_=res[g][:, cols].rearrange("p (i m) -> p i m", i=count),
                    )

            absolute(0)
            absolute(1)
            inverse_root(0, whole)
            absolute(2)
            inverse_root(1, whole)
            if last_part:
                inverse_root(2, tiles)
                square(2, tiles)
                for g in (0, 1):
                    once(g, tiles)
                    finish(g, tiles, False)
                finish(2, tiles, True)
            else:
                square(0, whole)
                inverse_root(2, whole)
                square(1, tiles[:1])
                once(2, whole)
                finish(0, whole, True)
                finish(2, whole, False)
                once(1, tiles[1:])
                finish(1, tiles[:1], True)
                finish(1, tiles[1:], False)
